import numpy as np
import ml_dtypes


def mxq(x, axis, fmt="e4m3"):
    dtype, down = {"e4m3": (ml_dtypes.float8_e4m3fn, 7), "e5m2": (ml_dtypes.float8_e5m2, 14)}[fmt]
    v = np.moveaxis(np.asarray(x, np.float32).astype(ml_dtypes.bfloat16).astype(np.float64), axis, -1)
    blocks = v.reshape(v.shape[:-1] + (-1, 32))
    amax = np.abs(blocks).max(-1, keepdims=True)
    byte = np.maximum(np.where(amax > 0, np.frexp(amax)[1] - 1 + 127, 0) - down, 1)
    scale = np.exp2(byte - 127.0)
    codes = (blocks / scale).astype(np.float32).astype(dtype).astype(np.float64)
    return np.moveaxis((codes * scale).reshape(v.shape), -1, axis)


WIDE = False


def mx_kscale(k):
    if not WIDE:
        return np.ones(k)
    levels = np.array([10, -10, 5, -5, 0])
    if k % 512:
        return np.exp2(np.random.permutation(np.resize(levels, k // 32))).repeat(32)
    a = np.empty((k // 512, 16))
    for p in range(k // 512):
        a[p, :8] = np.random.permutation(np.resize(levels, 8))
        for g in range(8):
            far = levels[np.abs(levels - a[p, g]) >= 10]
            a[p, g + 8] = far[np.random.randint(len(far))]
    return np.exp2(a.ravel()).repeat(32)


def f64(x):
    return np.asarray(x).astype(np.float64)


def striped(idx):
    return np.tile(idx.reshape(-1, 16).T, (8, 1)).astype(np.uint16)


def unstriped(offs):
    return offs[:16].T.reshape(-1).astype(np.int64)


def striped8(idx):
    return np.concatenate([x.reshape(-1, 16).T for x in idx]).astype(np.uint16)


def runs(offs, k):
    lists = np.stack([offs[16 * r : 16 * r + 16].T.reshape(-1) for r in range(8)]).astype(np.int64)
    return lists[np.arange(k) % 512 // 64]


def pack_weight(w):
    k, n = w.shape
    w = f64(np.asarray(w, np.float32).astype(ml_dtypes.bfloat16)).reshape(k // 32, 32, n)
    amax = np.abs(w).max(1)
    byte = np.clip(np.where(amax > 0, np.frexp(amax)[1] - 1 + 127 - 7, 1), 1, 254)
    scaled = (w * np.exp2(127.0 - byte)[:, None, :]).reshape(k, n).astype(np.float32)
    words = np.ascontiguousarray(scaled.reshape(k // 512, 128, 4, n).transpose(0, 1, 3, 2)).astype(ml_dtypes.float8_e4m3fn).view(np.uint8)
    return words, np.ascontiguousarray(byte.astype(np.uint8).reshape(k // 512, 16, n))


def unpack_weight(words, scales):
    g, p, n, _ = words.shape
    vals = np.ascontiguousarray(words).view(ml_dtypes.float8_e4m3fn).astype(np.float64) * np.repeat(np.exp2(scales.astype(np.float64) - 127.0), 8, axis=1)[..., None]
    return vals.transpose(0, 1, 3, 2).reshape(g * 512, n)


E2M1 = np.array([0.0, 0.5, 1.0, 1.5, 2.0, 3.0, 4.0, 6.0, -0.0, -0.5, -1.0, -1.5, -2.0, -3.0, -4.0, -6.0])


def pack_fp4(w):
    k, n = w.shape
    w = f64(np.asarray(w, np.float32).astype(ml_dtypes.bfloat16)).reshape(k // 32, 32, n)
    amax = np.abs(w).max(1)
    mant, ex = np.frexp(amax / 6.0)
    byte = np.clip(np.where(amax > 0, np.where(mant > 0.5, ex, ex - 1) + 127, 1), 1, 254)
    scaled = (w * np.exp2(127.0 - byte)[:, None, :]).reshape(k, n).astype(np.float32)
    c = np.ascontiguousarray(scaled.reshape(k // 512, 128, 4, n).transpose(0, 1, 3, 2)).astype(ml_dtypes.float4_e2m1fn).view(np.uint8) & 0xF
    words = (c[..., 0::2] | (c[..., 1::2] << 4)).reshape(k // 512, 128, 2 * n)
    return np.ascontiguousarray(words), np.ascontiguousarray(byte.astype(np.uint8).reshape(k // 512, 16, n))


def unpack_fp4(words, scales):
    g, _, n = scales.shape
    words = np.ascontiguousarray(words).reshape(g, 128, n, 2)
    nib = np.empty((g, 128, n, 4), np.uint8)
    nib[..., 0::2] = words & 0xF
    nib[..., 1::2] = words >> 4
    vals = E2M1[nib] * np.repeat(np.exp2(scales.astype(np.float64) - 127.0), 8, axis=1)[..., None]
    return vals.transpose(0, 1, 3, 2).reshape(g * 512, n)


def planes(y):
    n, m = y.shape
    v = y.astype(np.float32).astype(ml_dtypes.bfloat16).astype(np.float64).reshape(n // 32, 32, m)
    top = np.abs(v).max(1)
    byte = np.clip(np.where(top > 0, np.frexp(top)[1] - 1 + 127 - 7, 1), 1, 254)
    codes = (v * np.exp2(127.0 - byte)[:, None, :]).reshape(n, m).astype(np.float32).astype(ml_dtypes.float8_e4m3fn).view(np.uint8)
    words = codes.reshape(n // 512, 128, 4, m).transpose(0, 1, 3, 2)
    return np.ascontiguousarray(words), np.ascontiguousarray(byte.astype(np.uint8).reshape(n // 512, 16, m))


K, T, S, V, N, H = 512, 2048, 512, 256, 512, 512


def setup_inputs():
    n = np.random.standard_normal
    s = mx_kscale(K)[:, None]
    u = mx_kscale(H)
    packed_xT = pack_weight(n((K, T)) * s)
    packed_w1 = pack_fp4(n((K, H)) / np.sqrt(K) / s)
    packed_w2 = pack_fp4(n((H, H)) / np.sqrt(H) / u[:, None])
    packed_w3 = pack_fp4(n((H, N)) / np.sqrt(H) / u[:, None])
    return {
        "x_words": packed_xT[0],
        "x_scales": packed_xT[1],
        "w1_words": packed_w1[0],
        "w1_scales": packed_w1[1],
        "gn": (np.random.uniform(0.5, 1.5, (H, 1)) * u[:, None]).astype(np.float32),
        "w2_words": packed_w2[0],
        "w2_scales": packed_w2[1],
        "w3_words": packed_w3[0],
        "w3_scales": packed_w3[1],
        "offs": striped(np.random.permutation(T)[:S]),
        "src": striped8(np.stack([np.random.permutation(S)[:V] for _ in range(8)])),
        "dst": striped8(np.stack([np.random.permutation(S)[:V] for _ in range(8)])),
    }


def reference(x_words, x_scales, w1_words, w1_scales, gn, w2_words, w2_scales, w3_words, w3_scales, offs, src, dst):
    xq = unpack_weight(x_words, x_scales)[:, unstriped(offs)]
    y = unpack_fp4(w1_words, w1_scales).T @ xq
    z = f64(gn) * y
    h = np.tanh(unpack_fp4(w2_words, w2_scales).T @ mxq(z, 0, "e4m3"))
    m1 = h[np.arange(H)[:, None], runs(src, H)]
    p = y.copy()
    p[np.arange(H)[:, None], runs(dst, H)] = m1
    z2 = f64(gn) * p
    out_0 = unpack_fp4(w3_words, w3_scales).T @ mxq(z2, 0, "e4m3")
    return (out_0,) + planes(out_0)

@@ -1,0 +1,194 @@
+from contextlib import ExitStack
+
+import concourse.mybir as mybir
+
+K, T, S, V, H, N = 512, 2048, 512, 256, 512, 512
+FLOPS = 2 * S * (K * H + H * H + H * N)
+
+F32 = mybir.dt.float32
+BF16 = mybir.dt.bfloat16
+I32 = mybir.dt.int32
+U32 = mybir.dt.uint32
+U16 = mybir.dt.uint16
+U8 = mybir.dt.uint8
+FP8X4 = mybir.dt.float8_e4m3fn_x4
+FP4X4 = mybir.dt.float4_e2m1fn_x4
+ACT = mybir.ActivationFunctionType
+MULT = mybir.AluOpType.mult
+
+P = 128
+PACK = 4
+CH = 128
+NCH = S // CH
+HALF = 256
+
+
+def load_scale_rows(queues, plane, scales, quadrants):
+    for queue, q in zip(queues, quadrants):
+        queue.dma_start(out=plane[32 * q : 32 * q + 4, :].bitcast(I32), in_=scales[0, 4 * q : 4 * q + 4, :].bitcast(I32))
+
+
+def deal_words(nc, dealt, raw):
+    nc.vector.tensor_copy(
+        out=dealt[:].rearrange("p (t m b) -> p t m b", t=PACK, b=2),
+        in_=raw[:].rearrange("p (m t b) -> p t m b", t=PACK, b=2),
+    )
+
+
+def deal_scales(nc, dealt, raw):
+    nc.vector.tensor_copy(
+        out=dealt[:].rearrange("p (t m) -> p t m", t=PACK),
+        in_=raw[:].rearrange("p (m t) -> p t m", t=PACK),
+    )
+
+
+def product(nc, out, w_dealt, ws_dealt, t, codes, scales):
+    nc.tensor.matmul_mx(
+        out=out,
+        lhsT=w_dealt[:, 2 * P * t : 2 * P * (t + 1)].bitcast(FP4X4),
+        lhsT_scale=ws_dealt[:, P * t : P * (t + 1)],
+        rhs=codes.bitcast(FP8X4),
+        rhs_scale=scales,
+        start=True,
+        stop=True,
+    )
+
+
+def tile_picked_delivmat_none_po_kernel(
+    tc, x_words, x_scales, w1_words, w1_scales, gn, w2_words, w2_scales, w3_words, w3_scales, offs, src, dst, out_0, out_1, out_2
+):
+    nc = tc.nc
+    with ExitStack() as ctx:
+        sb = ctx.enter_context(tc.tile_pool(name="sb", bufs=1))
+        ps = ctx.enter_context(tc.psum_pool(name="ps", bufs=1))
+
+        offs_t = sb.tile([P, S // 16], U16, name="offs_t")
+        src_t = sb.tile([P, V // 16], U16, name="src_t")
+        dst_t = sb.tile([P, V // 16], U16, name="dst_t")
+        xw = sb.tile([P, T], U32, name="xw", align_bytes=64)
+        xs = sb.tile([P, T], U8, name="xs", tag="xs", align_bytes=64)
+        gain = sb.tile([P, PACK], F32, name="gain")
+        w_raw = [sb.tile([P, 2 * H], U8, name="w_raw0", tag="w_raw", align_bytes=64)]
+        ws_raw = [sb.tile([P, H], U8, name="ws_raw0", align_bytes=64)]
+        w_dealt = [sb.tile([P, 2 * H], U8, name="w_dealt0", align_bytes=64)]
+        ws_dealt = [sb.tile([P, H], U8, name="ws_dealt0", align_bytes=64)]
+
+        nc.vector.memset(xs[:].bitcast(I32), 0)
+        nc.vector.memset(ws_raw[0][:].bitcast(I32), 0)
+
+        nc.sync.dma_start(offs_t[:], offs)
+        nc.sync.dma_start(src_t[:], src)
+        nc.sync.dma_start(dst_t[:], dst)
+        nc.sync.dma_start(out=w_raw[0][:].bitcast(I32), in_=w1_words[0].bitcast(I32))
+        nc.sync.dma_start(out=xw[:].bitcast(I32), in_=x_words[0].rearrange("p c r -> p (c r)").bitcast(I32))
+        load_scale_rows([nc.scalar] * 3 + [nc.gpsimd], xs, x_scales, range(4))
+        load_scale_rows([nc.scalar] * 3 + [nc.gpsimd], ws_raw[0], w1_scales, range(4))
+        nc.gpsimd.dma_start(out=gain[:], in_=gn.rearrange("(p t) o -> p (t o)", t=PACK))
+
+        warm = sb.tile([P, 1], F32, name="warm")
+        nc.scalar.activation(warm[:], gain[:, 0:1], ACT.Tanh)
+
+        deal_words(nc, w_dealt[0], w_raw[0])
+        w_raw.append(sb.tile([P, 2 * H], U8, name="w_raw1", tag="w_raw", align_bytes=64))
+        nc.sync.dma_start(out=w_raw[1][:].bitcast(I32), in_=w2_words[0].bitcast(I32))
+        gs = sb.tile([P, S], U8, name="gs", tag="gs", align_bytes=64)
+        nc.vector.tensor_copy(gs[:], xs[:].indirect(offs_t[:]))
+        ws_raw.append(sb.tile([P, H], U8, name="ws_raw1", tag="xs", align_bytes=64))
+        nc.vector.memset(ws_raw[1][:].bitcast(I32), 0)
+        load_scale_rows([nc.sync] * 4, ws_raw[1], w2_scales, range(4))
+        gw = [sb.tile([P, HALF], U32, name="gw%d" % h, tag="gw%d" % h, align_bytes=64) for h in range(2)]
+        for h in range(2):
+            nc.vector.tensor_copy(gw[h][:], xw[:].indirect(offs_t[:, h * HALF // 16 : (h + 1) * HALF // 16]))
+            if h == 0:
+                deal_scales(nc, ws_dealt[0], ws_raw[0])
+        load_scale_rows([nc.sync] * 4, ws_raw[0], w3_scales, range(4))
+
+        y_ps = [ps.tile([P, PACK, CH], F32, name="y_ps%d" % c, tag="lo%d" % c) for c in range(NCH)]
+        for c in range(NCH):
+            h, r = divmod(c, 2)
+            for t in range(PACK):
+                product(nc, y_ps[c][:, t, :], w_dealt[0], ws_dealt[0], t, gw[h][:, r * CH : (r + 1) * CH], gs[:, c * CH : (c + 1) * CH])
+
+        z = [sb.tile([P, CH, PACK], BF16, name="z%d" % c, tag="z%d" % c, align_bytes=64) for c in range(NCH)]
+        zc = [sb.tile([P, CH], U32, name="zc%d" % c, tag="zc%d" % c, align_bytes=64) for c in range(NCH)]
+        zs = [sb.tile([P, CH], U8, name="zs%d" % c, tag="zs%d" % c, align_bytes=64) for c in range(NCH)]
+        a_ps = [ps.tile([P, S], F32, name="a_ps%d" % t, tag="hi%d" % t) for t in range(PACK)]
+        gain_b = gain[:].unsqueeze(1).to_broadcast([P, CH, PACK])
+
+        def scale(c):
+            nc.vector.tensor_tensor(z[c][:], y_ps[c][:].rearrange("p t j -> p j t"), gain_b, MULT)
+
+        def quantise(c):
+            nc.vector.quantize_mx(out=zc[c][:].bitcast(FP8X4), scales=zs[c][:], in_=z[c][:].rearrange("p j t -> p (j t)"))
+
+        scale(0)
+        w_dealt.append(sb.tile([P, 2 * H], U8, name="w_dealt1", tag="gw0", align_bytes=64))
+        deal_words(nc, w_dealt[1], w_raw[1])
+        w_raw.append(sb.tile([P, 2 * H], U8, name="w_raw2", tag="w_raw", align_bytes=64))
+        nc.sync.dma_start(out=w_raw[2][:].bitcast(I32), in_=w3_words[0].bitcast(I32))
+        scale(1)
+        quantise(0)
+        ws_dealt.append(sb.tile([P, H], U8, name="ws_dealt1", tag="gs", align_bytes=64))
+        deal_scales(nc, ws_dealt[1], ws_raw[1])
+        scale(2)
+        quantise(1)
+        scale(3)
+        quantise(2)
+        quantise(3)
+        for c in range(NCH):
+            for t in range(PACK):
+                product(nc, a_ps[t][:, c * CH : (c + 1) * CH], w_dealt[1], ws_dealt[1], t, zc[c][:], zs[c][:])
+
+        w_dealt.append(sb.tile([P, 2 * H], U8, name="w_dealt2", tag="z3", align_bytes=64))
+        ws_dealt.append(sb.tile([P, H], U8, name="ws_dealt2", tag="zs3", align_bytes=64))
+        deal_words(nc, w_dealt[2], w_raw[2])
+        deal_scales(nc, ws_dealt[2], ws_raw[0])
+
+        state = [sb.tile([P, S], F32, name="state0", tag="zc3", align_bytes=64)]
+        state.extend(sb.tile([P, S], F32, name="state%d" % t) for t in range(1, PACK))
+        hid = [sb.tile([P, S], F32, name="hid%d" % t) for t in range(PACK)]
+        msg = [sb.tile([P, V], F32, name="msg%d" % t) for t in range(PACK)]
+        z2 = [sb.tile([P, CH, PACK], BF16, name="z2_%d" % c, align_bytes=64) for c in range(NCH)]
+        for t in range(PACK):
+            nc.scalar.activation(hid[t][:], a_ps[t][:], ACT.Tanh)
+        for t in (1, 2, 3, 0):
+            for c in range(NCH):
+                nc.scalar.copy(state[t][:, c * CH : (c + 1) * CH], y_ps[c][:, t, :])
+        for t in range(PACK):
+            nc.vector.tensor_copy(msg[t][:], hid[t][:].indirect(src_t[:]))
+        for t in range(PACK):
+            nc.vector.tensor_copy(state[t][:].indirect(dst_t[:]), msg[t][:])
+            for c in range(NCH):
+                nc.scalar.activation(z2[c][:, :, t], state[t][:, c * CH : (c + 1) * CH], ACT.Copy, scale=gain[:, t : t + 1])
+
+        z2c = [sb.tile([P, CH], U32, name="z2c%d" % c, align_bytes=64) for c in range(NCH)]
+        z2s = [sb.tile([P, CH], U8, name="z2s%d" % c, align_bytes=64) for c in range(NCH)]
+        o_ps = [ps.tile([P, PACK, CH], F32, name="o_ps%d" % c, tag="lo%d" % c) for c in range(NCH)]
+        o32 = [sb.tile([P, PACK, CH], F32, name="o32_%d" % c) for c in range(NCH)]
+        o16 = [sb.tile([P, CH, PACK], BF16, name="o16_%d" % c, align_bytes=64) for c in range(NCH)]
+        oc = sb.tile([P, S], U32, name="oc", align_bytes=64)
+        osc = sb.tile([P, S], U8, name="osc", align_bytes=64)
+        out_rows = out_0.rearrange("(p t) j -> p t j", t=PACK)
+        out_words = out_1[0].rearrange("p c r -> p (c r)").bitcast(I32)
+        for c in range(NCH):
+            nc.vector.quantize_mx(out=z2c[c][:].bitcast(FP8X4), scales=z2s[c][:], in_=z2[c][:].rearrange("p j t -> p (j t)"))
+            for t in range(PACK):
+                product(nc, o_ps[c][:, t, :], w_dealt[2], ws_dealt[2], t, z2c[c][:], z2s[c][:])
+        for c in range(NCH):
+            cols = slice(c * CH, (c + 1) * CH)
+            if c == 0:
+                nc.vector.tensor_copy(o32[c][:], o_ps[c][:])
+            else:
+                nc.scalar.copy(o32[c][:], o_ps[c][:])
+            nc.sync.dma_start(out=out_rows[:, :, cols], in_=o32[c][:])
+            nc.vector.tensor_copy(
+                out=o16[c][:].rearrange("p (j i) t -> p j t i", i=4),
+                in_=o32[c][:].rearrange("p t (j i) -> p j t i", i=4),
+            )
+            nc.vector.quantize_mx(out=oc[:, cols].bitcast(FP8X4), scales=osc[:, cols], in_=o16[c][:].rearrange("p j t -> p (j t)"))
+            if c % 2 == 1:
+                half = slice((c - 1) * CH, (c + 1) * CH)
+                nc.sync.dma_start(out=out_words[:, half], in_=oc[:, half].bitcast(I32))
+        for q in range(4):
+            queue = nc.sync if q % 2 == 0 else nc.scalar
+            queue.dma_start(out=out_2[0, 4 * q : 4 * q + 4, :].bitcast(I32), in_=osc[32 * q : 32 * q + 4, :].bitcast(I32))

@@ -68,34 +68,36 @@ def tile_picked_delivmat_none_po_kernel(
         xw = sb.tile([P, T], U32, name="xw", align_bytes=64)
         xs = sb.tile([P, T], U8, name="xs", tag="xs", align_bytes=64)
         gain = sb.tile([P, PACK], F32, name="gain")
-        w_raw = [sb.tile([P, 2 * H], U8, name="w_raw0", tag="w_raw", align_bytes=64)]
+        w_raw = [sb.tile([P, 2 * H], U8, name="w_raw%d" % i, tag="w_raw%d" % i, align_bytes=64) for i in range(2)]
         ws_raw = [sb.tile([P, H], U8, name="ws_raw0", align_bytes=64)]
-        w_dealt = [sb.tile([P, 2 * H], U8, name="w_dealt0", align_bytes=64)]
+        w_dealt = [sb.tile([P, 2 * H], U8, name="w_dealt%d" % i, tag="w_dealt%d" % i, align_bytes=64) for i in range(2)]
         ws_dealt = [sb.tile([P, H], U8, name="ws_dealt0", align_bytes=64)]
 
         nc.vector.memset(xs[:].bitcast(I32), 0)
         nc.vector.memset(ws_raw[0][:].bitcast(I32), 0)
 
+        nc.scalar.dma_start(out=w_raw[0][:].bitcast(I32), in_=w1_words[0].bitcast(I32))
         nc.sync.dma_start(offs_t[:], offs)
+        nc.scalar.dma_start(out=w_raw[1][:].bitcast(I32), in_=w2_words[0].bitcast(I32))
         nc.sync.dma_start(src_t[:], src)
         nc.sync.dma_start(dst_t[:], dst)
-        nc.sync.dma_start(out=w_raw[0][:].bitcast(I32), in_=w1_words[0].bitcast(I32))
         nc.sync.dma_start(out=xw[:].bitcast(I32), in_=x_words[0].rearrange("p c r -> p (c r)").bitcast(I32))
-        load_scale_rows([nc.scalar] * 3 + [nc.gpsimd], xs, x_scales, range(4))
+        load_scale_rows([nc.scalar] * 4, xs, x_scales, range(4))
         load_scale_rows([nc.scalar] * 3 + [nc.gpsimd], ws_raw[0], w1_scales, range(4))
-        nc.gpsimd.dma_start(out=gain[:], in_=gn.rearrange("(p t) o -> p (t o)", t=PACK))
 
+        nc.gpsimd.dma_start(out=gain[:], in_=gn.rearrange("(p t) o -> p (t o)", t=PACK))
         warm = sb.tile([P, 1], F32, name="warm")
         nc.scalar.activation(warm[:], gain[:, 0:1], ACT.Tanh)
 
         deal_words(nc, w_dealt[0], w_raw[0])
-        w_raw.append(sb.tile([P, 2 * H], U8, name="w_raw1", tag="w_raw", align_bytes=64))
-        nc.sync.dma_start(out=w_raw[1][:].bitcast(I32), in_=w2_words[0].bitcast(I32))
-        gs = sb.tile([P, S], U8, name="gs", tag="gs", align_bytes=64)
-        nc.vector.tensor_copy(gs[:], xs[:].indirect(offs_t[:]))
-        ws_raw.append(sb.tile([P, H], U8, name="ws_raw1", tag="xs", align_bytes=64))
+        ws_raw.append(sb.tile([P, H], U8, name="ws_raw1", tag="w_raw0", align_bytes=64))
         nc.vector.memset(ws_raw[1][:].bitcast(I32), 0)
         load_scale_rows([nc.sync] * 4, ws_raw[1], w2_scales, range(4))
+        deal_words(nc, w_dealt[1], w_raw[1])
+        w_raw.append(sb.tile([P, 2 * H], U8, name="w_raw2", tag="w_raw1", align_bytes=64))
+        nc.sync.dma_start(out=w_raw[2][:].bitcast(I32), in_=w3_words[0].bitcast(I32))
+        gs = sb.tile([P, S], U8, name="gs", align_bytes=64)
+        nc.vector.tensor_copy(gs[:], xs[:].indirect(offs_t[:]))
         gw = [sb.tile([P, HALF], U32, name="gw%d" % h, tag="gw%d" % h, align_bytes=64) for h in range(2)]
         for h in range(2):
             nc.vector.tensor_copy(gw[h][:], xw[:].indirect(offs_t[:, h * HALF // 16 : (h + 1) * HALF // 16]))
@@ -122,44 +124,53 @@ def tile_picked_delivmat_none_po_kernel(
             nc.vector.quantize_mx(out=zc[c][:].bitcast(FP8X4), scales=zs[c][:], in_=z[c][:].rearrange("p j t -> p (j t)"))
 
         scale(0)
-        w_dealt.append(sb.tile([P, 2 * H], U8, name="w_dealt1", tag="gw0", align_bytes=64))
-        deal_words(nc, w_dealt[1], w_raw[1])
-        w_raw.append(sb.tile([P, 2 * H], U8, name="w_raw2", tag="w_raw", align_bytes=64))
-        nc.sync.dma_start(out=w_raw[2][:].bitcast(I32), in_=w3_words[0].bitcast(I32))
-        scale(1)
-        quantise(0)
-        ws_dealt.append(sb.tile([P, H], U8, name="ws_dealt1", tag="gs", align_bytes=64))
+        for t in range(PACK):
+            nc.scalar.activation(z[1][:, :, t], y_ps[1][:, t, :], ACT.Copy, scale=gain[:, t : t + 1])
+        ws_dealt.append(sb.tile([P, H], U8, name="ws_dealt1", tag="gw0", align_bytes=64))
         deal_scales(nc, ws_dealt[1], ws_raw[1])
+        quantise(0)
         scale(2)
-        quantise(1)
         scale(3)
         quantise(2)
+        quantise(1)
         quantise(3)
-        for c in range(NCH):
-            for t in range(PACK):
+        for t in range(PACK):
+            for c in (0, 2, 1, 3):
                 product(nc, a_ps[t][:, c * CH : (c + 1) * CH], w_dealt[1], ws_dealt[1], t, zc[c][:], zs[c][:])
 
         w_dealt.append(sb.tile([P, 2 * H], U8, name="w_dealt2", tag="z3", align_bytes=64))
-        ws_dealt.append(sb.tile([P, H], U8, name="ws_dealt2", tag="zs3", align_bytes=64))
         deal_words(nc, w_dealt[2], w_raw[2])
-        deal_scales(nc, ws_dealt[2], ws_raw[0])
 
-        state = [sb.tile([P, S], F32, name="state0", tag="zc3", align_bytes=64)]
-        state.extend(sb.tile([P, S], F32, name="state%d" % t) for t in range(1, PACK))
-        hid = [sb.tile([P, S], F32, name="hid%d" % t) for t in range(PACK)]
+        state = [
+            sb.tile([P, S], F32, name="state0"),
+            sb.tile([P, S], F32, name="state1", tag="w_dealt1", align_bytes=64),
+            sb.tile([P, S], F32, name="state2", tag="zc3", align_bytes=64),
+            sb.tile([P, S], F32, name="state3", tag="zs3", align_bytes=64),
+        ]
+        hid = [sb.tile([P, S], F32, name="hid%d" % t, tag="hid%d" % t, align_bytes=64) for t in range(PACK)]
         msg = [sb.tile([P, V], F32, name="msg%d" % t) for t in range(PACK)]
         z2 = [sb.tile([P, CH, PACK], BF16, name="z2_%d" % c, align_bytes=64) for c in range(NCH)]
         for t in range(PACK):
             nc.scalar.activation(hid[t][:], a_ps[t][:], ACT.Tanh)
-        for t in (1, 2, 3, 0):
-            for c in range(NCH):
+        for t in range(PACK):
+            for c in (0, 2, 1, 3):
                 nc.scalar.copy(state[t][:, c * CH : (c + 1) * CH], y_ps[c][:, t, :])
-        for t in range(PACK):
+
+        def fetch(t):
             nc.vector.tensor_copy(msg[t][:], hid[t][:].indirect(src_t[:]))
-        for t in range(PACK):
+
+        def deliver(t):
             nc.vector.tensor_copy(state[t][:].indirect(dst_t[:]), msg[t][:])
             for c in range(NCH):
                 nc.scalar.activation(z2[c][:, :, t], state[t][:, c * CH : (c + 1) * CH], ACT.Copy, scale=gain[:, t : t + 1])
+
+        fetch(0)
+        ws_dealt.append(sb.tile([P, H], U8, name="ws_dealt2", tag="hid0", align_bytes=64))
+        deal_scales(nc, ws_dealt[2], ws_raw[0])
+        for t in range(1, PACK):
+            fetch(t)
+            deliver(t - 1)
+        deliver(PACK - 1)
 
         z2c = [sb.tile([P, CH], U32, name="z2c%d" % c, align_bytes=64) for c in range(NCH)]
         z2s = [sb.tile([P, CH], U8, name="z2s%d" % c, align_bytes=64) for c in range(NCH)]

@@ -69,7 +69,7 @@ def tile_picked_delivmat_none_po_kernel(
         xs = sb.tile([P, T], U8, name="xs", tag="xs", align_bytes=64)
         gain = sb.tile([P, PACK], F32, name="gain")
         w_raw = [sb.tile([P, 2 * H], U8, name="w_raw%d" % i, tag="w_raw%d" % i, align_bytes=64) for i in range(2)]
-        ws_raw = [sb.tile([P, H], U8, name="ws_raw0", align_bytes=64)]
+        ws_raw = [sb.tile([P, H], U8, name="ws_raw0", tag="ws_raw0", align_bytes=64)]
         w_dealt = [sb.tile([P, 2 * H], U8, name="w_dealt%d" % i, tag="w_dealt%d" % i, align_bytes=64) for i in range(2)]
         ws_dealt = [sb.tile([P, H], U8, name="ws_dealt0", align_bytes=64)]
 
@@ -96,29 +96,31 @@ def tile_picked_delivmat_none_po_kernel(
         deal_words(nc, w_dealt[1], w_raw[1])
         w_raw.append(sb.tile([P, 2 * H], U8, name="w_raw2", tag="w_raw1", align_bytes=64))
         nc.sync.dma_start(out=w_raw[2][:].bitcast(I32), in_=w3_words[0].bitcast(I32))
-        gs = sb.tile([P, S], U8, name="gs", align_bytes=64)
-        nc.vector.tensor_copy(gs[:], xs[:].indirect(offs_t[:]))
         gw = [sb.tile([P, HALF], U32, name="gw%d" % h, tag="gw%d" % h, align_bytes=64) for h in range(2)]
-        for h in range(2):
-            nc.vector.tensor_copy(gw[h][:], xw[:].indirect(offs_t[:, h * HALF // 16 : (h + 1) * HALF // 16]))
-            if h == 0:
-                deal_scales(nc, ws_dealt[0], ws_raw[0])
-        load_scale_rows([nc.sync] * 4, ws_raw[0], w3_scales, range(4))
+        gs = [sb.tile([P, HALF], U8, name="gs0", align_bytes=64)]
+        nc.vector.tensor_copy(gw[0][:], xw[:].indirect(offs_t[:, : HALF // 16]))
+        nc.vector.tensor_copy(gs[0][:], xs[:].indirect(offs_t[:, : HALF // 16]))
+        deal_scales(nc, ws_dealt[0], ws_raw[0])
+        gs.append(sb.tile([P, HALF], U8, name="gs1", tag="ws_raw0", align_bytes=64))
+        nc.vector.tensor_copy(gs[1][:], xs[:].indirect(offs_t[:, HALF // 16 :]))
+        nc.vector.tensor_copy(gw[1][:], xw[:].indirect(offs_t[:, HALF // 16 :]))
 
         y_ps = [ps.tile([P, PACK, CH], F32, name="y_ps%d" % c, tag="lo%d" % c) for c in range(NCH)]
         for c in range(NCH):
             h, r = divmod(c, 2)
             for t in range(PACK):
-                product(nc, y_ps[c][:, t, :], w_dealt[0], ws_dealt[0], t, gw[h][:, r * CH : (r + 1) * CH], gs[:, c * CH : (c + 1) * CH])
+                product(nc, y_ps[c][:, t, :], w_dealt[0], ws_dealt[0], t, gw[h][:, r * CH : (r + 1) * CH], gs[h][:, r * CH : (r + 1) * CH])
 
         z = [sb.tile([P, CH, PACK], BF16, name="z%d" % c, tag="z%d" % c, align_bytes=64) for c in range(NCH)]
         zc = [sb.tile([P, CH], U32, name="zc%d" % c, tag="zc%d" % c, align_bytes=64) for c in range(NCH)]
         zs = [sb.tile([P, CH], U8, name="zs%d" % c, tag="zs%d" % c, align_bytes=64) for c in range(NCH)]
         a_ps = [ps.tile([P, S], F32, name="a_ps%d" % t, tag="hi%d" % t) for t in range(PACK)]
-        gain_b = gain[:].unsqueeze(1).to_broadcast([P, CH, PACK])
+        gain_b = gain[:].unsqueeze(1).unsqueeze(3).to_broadcast([P, CH // 2, PACK, 2])
 
         def scale(c):
-            nc.vector.tensor_tensor(z[c][:], y_ps[c][:].rearrange("p t j -> p j t"), gain_b, MULT)
+            nc.vector.tensor_tensor(
+                z[c][:].rearrange("p (j i) t -> p j t i", i=2), y_ps[c][:].rearrange("p t (j i) -> p j t i", i=2), gain_b, MULT
+            )
 
         def quantise(c):
             nc.vector.quantize_mx(out=zc[c][:].bitcast(FP8X4), scales=zs[c][:], in_=z[c][:].rearrange("p j t -> p (j t)"))
@@ -128,6 +130,7 @@ def tile_picked_delivmat_none_po_kernel(
             nc.scalar.activation(z[1][:, :, t], y_ps[1][:, t, :], ACT.Copy, scale=gain[:, t : t + 1])
         ws_dealt.append(sb.tile([P, H], U8, name="ws_dealt1", tag="gw0", align_bytes=64))
         deal_scales(nc, ws_dealt[1], ws_raw[1])
+        load_scale_rows([nc.sync] * 4, ws_raw[1], w3_scales, range(4))
         quantise(0)
         scale(2)
         scale(3)
@@ -166,7 +169,7 @@ def tile_picked_delivmat_none_po_kernel(
 
         fetch(0)
         ws_dealt.append(sb.tile([P, H], U8, name="ws_dealt2", tag="hid0", align_bytes=64))
-        deal_scales(nc, ws_dealt[2], ws_raw[0])
+        deal_scales(nc, ws_dealt[2], ws_raw[1])
         for t in range(1, PACK):
             fetch(t)
             deliver(t - 1)
@@ -174,8 +177,11 @@ def tile_picked_delivmat_none_po_kernel(
 
         z2c = [sb.tile([P, CH], U32, name="z2c%d" % c, align_bytes=64) for c in range(NCH)]
         z2s = [sb.tile([P, CH], U8, name="z2s%d" % c, align_bytes=64) for c in range(NCH)]
-        o_ps = [ps.tile([P, PACK, CH], F32, name="o_ps%d" % c, tag="lo%d" % c) for c in range(NCH)]
-        o32 = [sb.tile([P, PACK, CH], F32, name="o32_%d" % c) for c in range(NCH)]
+        o_ps = [
+            [ps.tile([P, 2, CH], F32, name="o_ps%d_%d" % (c, u), tag=("lo%d", "hi%d")[u] % c) for u in range(2)] for c in range(NCH)
+        ]
+        o32_tail = sb.tile([P, PACK, 2 * CH], F32, name="o32_tail")
+        o32 = [sb.tile([P, PACK, CH], F32, name="o32_%d" % c)[:] for c in range(2)] + [o32_tail[:, :, :CH], o32_tail[:, :, CH:]]
         o16 = [sb.tile([P, CH, PACK], BF16, name="o16_%d" % c, align_bytes=64) for c in range(NCH)]
         oc = sb.tile([P, S], U32, name="oc", align_bytes=64)
         osc = sb.tile([P, S], U8, name="osc", align_bytes=64)
@@ -184,22 +190,26 @@ def tile_picked_delivmat_none_po_kernel(
         for c in range(NCH):
             nc.vector.quantize_mx(out=z2c[c][:].bitcast(FP8X4), scales=z2s[c][:], in_=z2[c][:].rearrange("p j t -> p (j t)"))
             for t in range(PACK):
-                product(nc, o_ps[c][:, t, :], w_dealt[2], ws_dealt[2], t, z2c[c][:], z2s[c][:])
+                product(nc, o_ps[c][t // 2][:, t % 2, :], w_dealt[2], ws_dealt[2], t, z2c[c][:], z2s[c][:])
         for c in range(NCH):
             cols = slice(c * CH, (c + 1) * CH)
-            if c == 0:
-                nc.vector.tensor_copy(o32[c][:], o_ps[c][:])
-            else:
-                nc.scalar.copy(o32[c][:], o_ps[c][:])
-            nc.sync.dma_start(out=out_rows[:, :, cols], in_=o32[c][:])
+            for u in range(2):
+                if c == 0:
+                    nc.vector.tensor_copy(o32[c][:, 2 * u : 2 * u + 2, :], o_ps[c][u][:])
+                else:
+                    nc.scalar.copy(o32[c][:, 2 * u : 2 * u + 2, :], o_ps[c][u][:])
+            if c < 2:
+                nc.sync.dma_start(out=out_rows[:, :, cols], in_=o32[c])
+            if c == 3:
+                nc.sync.dma_start(out=out_rows[:, :, 2 * CH :], in_=o32_tail[:])
             nc.vector.tensor_copy(
                 out=o16[c][:].rearrange("p (j i) t -> p j t i", i=4),
-                in_=o32[c][:].rearrange("p t (j i) -> p j t i", i=4),
+                in_=o32[c].rearrange("p t (j i) -> p j t i", i=4),
             )
             nc.vector.quantize_mx(out=oc[:, cols].bitcast(FP8X4), scales=osc[:, cols], in_=o16[c][:].rearrange("p j t -> p (j t)"))
-            if c % 2 == 1:
-                half = slice((c - 1) * CH, (c + 1) * CH)
-                nc.sync.dma_start(out=out_words[:, half], in_=oc[:, half].bitcast(I32))
+            if c >= 2:
+                done = slice(0, 3 * CH) if c == 2 else cols
+                nc.sync.dma_start(out=out_words[:, done], in_=oc[:, done].bitcast(I32))
         for q in range(4):
-            queue = nc.sync if q % 2 == 0 else nc.scalar
+            queue = nc.sync if q == 0 else nc.scalar
             queue.dma_start(out=out_2[0, 4 * q : 4 * q + 4, :].bitcast(I32), in_=osc[32 * q : 32 * q + 4, :].bitcast(I32))

@@ -96,13 +96,14 @@ def tile_picked_delivmat_none_po_kernel(
         deal_words(nc, w_dealt[1], w_raw[1])
         w_raw.append(sb.tile([P, 2 * H], U8, name="w_raw2", tag="w_raw1", align_bytes=64))
         nc.sync.dma_start(out=w_raw[2][:].bitcast(I32), in_=w3_words[0].bitcast(I32))
-        gw = [sb.tile([P, HALF], U32, name="gw%d" % h, tag="gw%d" % h, align_bytes=64) for h in range(2)]
+        gw = [sb.tile([P, HALF], U32, name="gw0", tag="gw0", align_bytes=64)]
         gs = [sb.tile([P, HALF], U8, name="gs0", align_bytes=64)]
         nc.vector.tensor_copy(gw[0][:], xw[:].indirect(offs_t[:, : HALF // 16]))
         nc.vector.tensor_copy(gs[0][:], xs[:].indirect(offs_t[:, : HALF // 16]))
         deal_scales(nc, ws_dealt[0], ws_raw[0])
         gs.append(sb.tile([P, HALF], U8, name="gs1", tag="ws_raw0", align_bytes=64))
         nc.vector.tensor_copy(gs[1][:], xs[:].indirect(offs_t[:, HALF // 16 :]))
+        gw.append(sb.tile([P, HALF], U32, name="gw1", tag="xs", align_bytes=64))
         nc.vector.tensor_copy(gw[1][:], xw[:].indirect(offs_t[:, HALF // 16 :]))
 
         y_ps = [ps.tile([P, PACK, CH], F32, name="y_ps%d" % c, tag="lo%d" % c) for c in range(NCH)]
@@ -112,7 +113,7 @@ def tile_picked_delivmat_none_po_kernel(
                 product(nc, y_ps[c][:, t, :], w_dealt[0], ws_dealt[0], t, gw[h][:, r * CH : (r + 1) * CH], gs[h][:, r * CH : (r + 1) * CH])
 
         z = [sb.tile([P, CH, PACK], BF16, name="z%d" % c, tag="z%d" % c, align_bytes=64) for c in range(NCH)]
-        zc = [sb.tile([P, CH], U32, name="zc%d" % c, tag="zc%d" % c, align_bytes=64) for c in range(NCH)]
+        zc = {c: sb.tile([P, CH], U32, name="zc%d" % c, tag="zc%d" % c, align_bytes=64) for c in range(1, NCH)}
         zs = [sb.tile([P, CH], U8, name="zs%d" % c, tag="zs%d" % c, align_bytes=64) for c in range(NCH)]
         a_ps = [ps.tile([P, S], F32, name="a_ps%d" % t, tag="hi%d" % t) for t in range(PACK)]
         gain_b = gain[:].unsqueeze(1).unsqueeze(3).to_broadcast([P, CH // 2, PACK, 2])
@@ -125,20 +126,21 @@ def tile_picked_delivmat_none_po_kernel(
         def quantise(c):
             nc.vector.quantize_mx(out=zc[c][:].bitcast(FP8X4), scales=zs[c][:], in_=z[c][:].rearrange("p j t -> p (j t)"))
 
-        scale(0)
         for t in range(PACK):
-            nc.scalar.activation(z[1][:, :, t], y_ps[1][:, t, :], ACT.Copy, scale=gain[:, t : t + 1])
+            nc.scalar.activation(z[0][:, :, t], y_ps[0][:, t, :], ACT.Copy, scale=gain[:, t : t + 1])
+        scale(1)
         ws_dealt.append(sb.tile([P, H], U8, name="ws_dealt1", tag="gw0", align_bytes=64))
         deal_scales(nc, ws_dealt[1], ws_raw[1])
         load_scale_rows([nc.sync] * 4, ws_raw[1], w3_scales, range(4))
-        quantise(0)
+        quantise(1)
         scale(2)
         scale(3)
         quantise(2)
-        quantise(1)
+        zc.setdefault(0, sb.tile([P, CH], U32, name="zc0", tag="z2", align_bytes=64))
+        quantise(0)
         quantise(3)
         for t in range(PACK):
-            for c in (0, 2, 1, 3):
+            for c in (1, 2, 0, 3):
                 product(nc, a_ps[t][:, c * CH : (c + 1) * CH], w_dealt[1], ws_dealt[1], t, zc[c][:], zs[c][:])
 
         w_dealt.append(sb.tile([P, 2 * H], U8, name="w_dealt2", tag="z3", align_bytes=64))
@@ -146,7 +148,7 @@ def tile_picked_delivmat_none_po_kernel(
 
         state = [
             sb.tile([P, S], F32, name="state0"),
-            sb.tile([P, S], F32, name="state1", tag="w_dealt1", align_bytes=64),
+            sb.tile([P, S], F32, name="state1"),
             sb.tile([P, S], F32, name="state2", tag="zc3", align_bytes=64),
             sb.tile([P, S], F32, name="state3", tag="zs3", align_bytes=64),
         ]
@@ -156,7 +158,7 @@ def tile_picked_delivmat_none_po_kernel(
         for t in range(PACK):
             nc.scalar.activation(hid[t][:], a_ps[t][:], ACT.Tanh)
         for t in range(PACK):
-            for c in (0, 2, 1, 3):
+            for c in (1, 2, 0, 3):
                 nc.scalar.copy(state[t][:, c * CH : (c + 1) * CH], y_ps[c][:, t, :])
 
         def fetch(t):

@@ -23,20 +23,20 @@ NCH = S // CH
 HALF = 256
 
 
-def load_scale_rows(queues, plane, scales, quadrants):
-    for queue, q in zip(queues, quadrants):
+def load_scale_rows(queues, plane, scales):
+    for q, queue in enumerate(queues):
         queue.dma_start(out=plane[32 * q : 32 * q + 4, :].bitcast(I32), in_=scales[0, 4 * q : 4 * q + 4, :].bitcast(I32))
 
 
-def deal_words(nc, dealt, raw):
-    nc.vector.tensor_copy(
+def deal_words(engine, dealt, raw):
+    engine.tensor_copy(
         out=dealt[:].rearrange("p (t m b) -> p t m b", t=PACK, b=2),
         in_=raw[:].rearrange("p (m t b) -> p t m b", t=PACK, b=2),
     )
 
 
-def deal_scales(nc, dealt, raw):
-    nc.vector.tensor_copy(
+def deal_scales(engine, dealt, raw):
+    engine.tensor_copy(
         out=dealt[:].rearrange("p (t m) -> p t m", t=PACK),
         in_=raw[:].rearrange("p (m t) -> p t m", t=PACK),
     )
@@ -82,25 +82,25 @@ def tile_picked_delivmat_none_po_kernel(
         nc.sync.dma_start(src_t[:], src)
         nc.sync.dma_start(dst_t[:], dst)
         nc.sync.dma_start(out=xw[:].bitcast(I32), in_=x_words[0].rearrange("p c r -> p (c r)").bitcast(I32))
-        load_scale_rows([nc.scalar] * 4, xs, x_scales, range(4))
-        load_scale_rows([nc.scalar] * 3 + [nc.gpsimd], ws_raw[0], w1_scales, range(4))
+        load_scale_rows([nc.scalar] * 4, xs, x_scales)
+        load_scale_rows([nc.scalar] * 3 + [nc.gpsimd], ws_raw[0], w1_scales)
 
         nc.gpsimd.dma_start(out=gain[:], in_=gn.rearrange("(p t) o -> p (t o)", t=PACK))
         warm = sb.tile([P, 1], F32, name="warm")
         nc.scalar.activation(warm[:], gain[:, 0:1], ACT.Tanh)
 
-        deal_words(nc, w_dealt[0], w_raw[0])
+        deal_words(nc.vector, w_dealt[0], w_raw[0])
         ws_raw.append(sb.tile([P, H], U8, name="ws_raw1", tag="w_raw0", align_bytes=64))
         nc.vector.memset(ws_raw[1][:].bitcast(I32), 0)
-        load_scale_rows([nc.sync] * 4, ws_raw[1], w2_scales, range(4))
-        deal_words(nc, w_dealt[1], w_raw[1])
+        load_scale_rows([nc.sync] * 4, ws_raw[1], w2_scales)
+        deal_words(nc.vector, w_dealt[1], w_raw[1])
         w_raw.append(sb.tile([P, 2 * H], U8, name="w_raw2", tag="w_raw1", align_bytes=64))
         nc.sync.dma_start(out=w_raw[2][:].bitcast(I32), in_=w3_words[0].bitcast(I32))
         gw = [sb.tile([P, HALF], U32, name="gw0", tag="gw0", align_bytes=64)]
         gs = [sb.tile([P, HALF], U8, name="gs0", align_bytes=64)]
         nc.vector.tensor_copy(gw[0][:], xw[:].indirect(offs_t[:, : HALF // 16]))
         nc.vector.tensor_copy(gs[0][:], xs[:].indirect(offs_t[:, : HALF // 16]))
-        deal_scales(nc, ws_dealt[0], ws_raw[0])
+        deal_scales(nc.vector, ws_dealt[0], ws_raw[0])
         gs.append(sb.tile([P, HALF], U8, name="gs1", tag="ws_raw0", align_bytes=64))
         nc.vector.tensor_copy(gs[1][:], xs[:].indirect(offs_t[:, HALF // 16 :]))
         gw.append(sb.tile([P, HALF], U32, name="gw1", tag="xs", align_bytes=64))
@@ -113,9 +113,17 @@ def tile_picked_delivmat_none_po_kernel(
                 product(nc, y_ps[c][:, t, :], w_dealt[0], ws_dealt[0], t, gw[h][:, r * CH : (r + 1) * CH], gs[h][:, r * CH : (r + 1) * CH])
 
         z = [sb.tile([P, CH, PACK], BF16, name="z%d" % c, tag="z%d" % c, align_bytes=64) for c in range(NCH)]
-        zc = {c: sb.tile([P, CH], U32, name="zc%d" % c, tag="zc%d" % c, align_bytes=64) for c in range(1, NCH)}
+        zc = [sb.tile([P, CH], U32, name="zc%d" % c, tag="zc%d" % c, align_bytes=64) for c in range(NCH)]
         zs = [sb.tile([P, CH], U8, name="zs%d" % c, tag="zs%d" % c, align_bytes=64) for c in range(NCH)]
-        a_ps = [ps.tile([P, S], F32, name="a_ps%d" % t, tag="hi%d" % t) for t in range(PACK)]
+        order = (2, 0, 1, 3)
+        a_ends = [ps.tile([P, 2, HALF], F32, name="a_ends%d" % h, tag="hi%d" % h) for h in range(2)]
+        a_mid = [ps.tile([P, 2, HALF], F32, name="a_mid%d" % i, tag="hi%d" % (2 + i)) for i in range(2)]
+        a_ps = {
+            order[0]: [a_ends[h][:, 0, :] for h in range(2)],
+            order[1]: [a_mid[0][:, h, :] for h in range(2)],
+            order[2]: [a_mid[1][:, h, :] for h in range(2)],
+            order[3]: [a_ends[h][:, 1, :] for h in range(2)],
+        }
         gain_b = gain[:].unsqueeze(1).unsqueeze(3).to_broadcast([P, CH // 2, PACK, 2])
 
         def scale(c):
@@ -126,87 +134,125 @@ def tile_picked_delivmat_none_po_kernel(
         def quantise(c):
             nc.vector.quantize_mx(out=zc[c][:].bitcast(FP8X4), scales=zs[c][:], in_=z[c][:].rearrange("p j t -> p (j t)"))
 
+        def second(t, c):
+            product(nc, a_ps[t][c // 2][:, c % 2 * CH : (c % 2 + 1) * CH], w_dealt[1], ws_dealt[1], t, zc[c][:], zs[c][:])
+
         for t in range(PACK):
             nc.scalar.activation(z[0][:, :, t], y_ps[0][:, t, :], ACT.Copy, scale=gain[:, t : t + 1])
-        scale(1)
         ws_dealt.append(sb.tile([P, H], U8, name="ws_dealt1", tag="gw0", align_bytes=64))
-        deal_scales(nc, ws_dealt[1], ws_raw[1])
-        load_scale_rows([nc.sync] * 4, ws_raw[1], w3_scales, range(4))
-        quantise(1)
+        scale(1)
+        deal_scales(nc.vector, ws_dealt[1], ws_raw[1])
+        load_scale_rows([nc.sync] * 4, ws_raw[1], w3_scales)
         scale(2)
+        quantise(1)
+        quantise(0)
         scale(3)
         quantise(2)
-        zc.setdefault(0, sb.tile([P, CH], U32, name="zc0", tag="z2", align_bytes=64))
-        quantise(0)
         quantise(3)
-        for t in range(PACK):
-            for c in (1, 2, 0, 3):
-                product(nc, a_ps[t][:, c * CH : (c + 1) * CH], w_dealt[1], ws_dealt[1], t, zc[c][:], zs[c][:])
 
-        w_dealt.append(sb.tile([P, 2 * H], U8, name="w_dealt2", tag="z3", align_bytes=64))
-        deal_words(nc, w_dealt[2], w_raw[2])
-
-        state = [
-            sb.tile([P, S], F32, name="state0"),
-            sb.tile([P, S], F32, name="state1"),
-            sb.tile([P, S], F32, name="state2", tag="zc3", align_bytes=64),
-            sb.tile([P, S], F32, name="state3", tag="zs3", align_bytes=64),
-        ]
+        state = {
+            order[0]: sb.tile([P, S], F32, name="state_a", tag="state_a"),
+            order[1]: sb.tile([P, S], F32, name="state_b"),
+            order[2]: sb.tile([P, S], F32, name="state_c", tag="zs3", align_bytes=64),
+        }
         hid = [sb.tile([P, S], F32, name="hid%d" % t, tag="hid%d" % t, align_bytes=64) for t in range(PACK)]
         msg = [sb.tile([P, V], F32, name="msg%d" % t) for t in range(PACK)]
         z2 = [sb.tile([P, CH, PACK], BF16, name="z2_%d" % c, align_bytes=64) for c in range(NCH)]
-        for t in range(PACK):
-            nc.scalar.activation(hid[t][:], a_ps[t][:], ACT.Tanh)
-        for t in range(PACK):
-            for c in (1, 2, 0, 3):
+
+        def fill(t, chunks):
+            for c in chunks:
                 nc.scalar.copy(state[t][:, c * CH : (c + 1) * CH], y_ps[c][:, t, :])
+
+        def tanh_half(t, h):
+            nc.scalar.activation(hid[t][:, h * HALF : (h + 1) * HALF], a_ps[t][h], ACT.Tanh)
+
+        def tanh_mid(i):
+            nc.scalar.activation(hid[order[1 + i]][:], a_mid[i][:].rearrange("p h j -> p (h j)"), ACT.Tanh)
 
         def fetch(t):
             nc.vector.tensor_copy(msg[t][:], hid[t][:].indirect(src_t[:]))
 
         def deliver(t):
             nc.vector.tensor_copy(state[t][:].indirect(dst_t[:]), msg[t][:])
-            for c in range(NCH):
+
+        def weave(t, chunks):
+            for c in chunks:
                 nc.scalar.activation(z2[c][:, :, t], state[t][:, c * CH : (c + 1) * CH], ACT.Copy, scale=gain[:, t : t + 1])
 
-        fetch(0)
-        ws_dealt.append(sb.tile([P, H], U8, name="ws_dealt2", tag="hid0", align_bytes=64))
-        deal_scales(nc, ws_dealt[2], ws_raw[1])
-        for t in range(1, PACK):
-            fetch(t)
-            deliver(t - 1)
-        deliver(PACK - 1)
+        for c in (1, 0):
+            for t in (order[0], order[3], order[1], order[2]):
+                second(t, c)
+        for t in order[:3]:
+            for c in (2, 3):
+                second(t, c)
+        tanh_half(order[0], 0)
+        tanh_half(order[0], 1)
+        for c in (2, 3):
+            second(order[3], c)
+        for c in range(NCH):
+            for t in order[:2]:
+                fill(t, [c])
+
+        w_dealt.append(sb.tile([P, 2 * H], U8, name="w_dealt2", tag="z3", align_bytes=64))
+        deal_words(nc.vector, w_dealt[2], w_raw[2])
+
+        tanh_mid(0)
+        tanh_mid(1)
+        tanh_half(order[3], 0)
+        tanh_half(order[3], 1)
+        fetch(order[0])
+        ws_dealt.append(sb.tile([P, H], U8, name="ws_dealt2", tag="hid%d" % order[0], align_bytes=64))
+        deal_scales(nc.vector, ws_dealt[2], ws_raw[1])
+        fetch(order[1])
+        deliver(order[0])
+        fetch(order[2])
+        deliver(order[1])
+        fill(order[2], range(NCH))
+        fetch(order[3])
+        deliver(order[2])
+        weave(order[0], range(NCH))
+        state.setdefault(order[3], sb.tile([P, S], F32, name="state_d", tag="state_a"))
+        fill(order[3], range(NCH))
+        weave(order[1], range(NCH))
+        deliver(order[3])
+        weave(order[2], range(NCH))
 
         z2c = [sb.tile([P, CH], U32, name="z2c%d" % c, align_bytes=64) for c in range(NCH)]
         z2s = [sb.tile([P, CH], U8, name="z2s%d" % c, align_bytes=64) for c in range(NCH)]
         o_ps = [
             [ps.tile([P, 2, CH], F32, name="o_ps%d_%d" % (c, u), tag=("lo%d", "hi%d")[u] % c) for u in range(2)] for c in range(NCH)
         ]
-        o32_tail = sb.tile([P, PACK, 2 * CH], F32, name="o32_tail")
-        o32 = [sb.tile([P, PACK, CH], F32, name="o32_%d" % c)[:] for c in range(2)] + [o32_tail[:, :, :CH], o32_tail[:, :, CH:]]
+        o32 = [sb.tile([P, PACK, CH], F32, name="o32_%d" % c) for c in range(NCH)]
         o16 = [sb.tile([P, CH, PACK], BF16, name="o16_%d" % c, align_bytes=64) for c in range(NCH)]
         oc = sb.tile([P, S], U32, name="oc", align_bytes=64)
         osc = sb.tile([P, S], U8, name="osc", align_bytes=64)
         out_rows = out_0.rearrange("(p t) j -> p t j", t=PACK)
         out_words = out_1[0].rearrange("p c r -> p (c r)").bitcast(I32)
-        for c in range(NCH):
+        last = order[3]
+
+        def weave_last(c):
+            nc.vector.tensor_scalar(z2[c][:, :, last], state[last][:, c * CH : (c + 1) * CH], gain[:, last : last + 1], None, MULT)
+
+        def third(c):
             nc.vector.quantize_mx(out=z2c[c][:].bitcast(FP8X4), scales=z2s[c][:], in_=z2[c][:].rearrange("p j t -> p (j t)"))
             for t in range(PACK):
                 product(nc, o_ps[c][t // 2][:, t % 2, :], w_dealt[2], ws_dealt[2], t, z2c[c][:], z2s[c][:])
+
+        weave_last(0)
+        weave(last, [1, 3])
+        weave_last(2)
+        third(0)
+        third(1)
+        third(2)
+        third(3)
         for c in range(NCH):
             cols = slice(c * CH, (c + 1) * CH)
             for u in range(2):
-                if c == 0:
-                    nc.vector.tensor_copy(o32[c][:, 2 * u : 2 * u + 2, :], o_ps[c][u][:])
-                else:
-                    nc.scalar.copy(o32[c][:, 2 * u : 2 * u + 2, :], o_ps[c][u][:])
-            if c < 2:
-                nc.sync.dma_start(out=out_rows[:, :, cols], in_=o32[c])
-            if c == 3:
-                nc.sync.dma_start(out=out_rows[:, :, 2 * CH :], in_=o32_tail[:])
+                nc.scalar.copy(o32[c][:, 2 * u : 2 * u + 2, :], o_ps[c][u][:])
+            nc.sync.dma_start(out=out_rows[:, :, cols], in_=o32[c][:])
             nc.vector.tensor_copy(
                 out=o16[c][:].rearrange("p (j i) t -> p j t i", i=4),
-                in_=o32[c].rearrange("p t (j i) -> p j t i", i=4),
+                in_=o32[c][:].rearrange("p t (j i) -> p j t i", i=4),
             )
             nc.vector.quantize_mx(out=oc[:, cols].bitcast(FP8X4), scales=osc[:, cols], in_=o16[c][:].rearrange("p j t -> p (j t)"))
             if c >= 2:

@@ -60,6 +60,7 @@ def tile_picked_delivmat_none_po_kernel(
     nc = tc.nc
     with ExitStack() as ctx:
         sb = ctx.enter_context(tc.tile_pool(name="sb", bufs=1))
+        stage = ctx.enter_context(tc.tile_pool(name="stage", bufs=1))
         ps = ctx.enter_context(tc.psum_pool(name="ps", bufs=1))
 
         offs_t = sb.tile([P, S // 16], U16, name="offs_t")
@@ -68,7 +69,7 @@ def tile_picked_delivmat_none_po_kernel(
         xw = sb.tile([P, T], U32, name="xw", align_bytes=64)
         xs = sb.tile([P, T], U8, name="xs", tag="xs", align_bytes=64)
         gain = sb.tile([P, PACK], F32, name="gain")
-        w_raw = [sb.tile([P, 2 * H], U8, name="w_raw%d" % i, tag="w_raw%d" % i, align_bytes=64) for i in range(2)]
+        w_raw = [stage.tile([P, 2 * H], U8, name="w_raw0", align_bytes=64, offset=896), sb.tile([P, 2 * H], U8, name="w_raw1", tag="w_raw1", align_bytes=64)]
         ws_raw = [sb.tile([P, H], U8, name="ws_raw0", tag="ws_raw0", align_bytes=64)]
         w_dealt = [sb.tile([P, 2 * H], U8, name="w_dealt%d" % i, tag="w_dealt%d" % i, align_bytes=64) for i in range(2)]
         ws_dealt = [sb.tile([P, H], U8, name="ws_dealt0", align_bytes=64)]
@@ -90,12 +91,14 @@ def tile_picked_delivmat_none_po_kernel(
         nc.scalar.activation(warm[:], gain[:, 0:1], ACT.Tanh)
 
         deal_words(nc.vector, w_dealt[0], w_raw[0])
-        ws_raw.append(sb.tile([P, H], U8, name="ws_raw1", tag="w_raw0", align_bytes=64))
-        nc.vector.memset(ws_raw[1][:].bitcast(I32), 0)
+        for i, offset in ((1, 1792), (2, 512)):
+            ws_raw.append(stage.tile([P, H], U8, name="ws_raw%d" % i, align_bytes=64, offset=offset))
+            nc.vector.memset(ws_raw[i][:].bitcast(I32), 0)
         load_scale_rows([nc.sync] * 4, ws_raw[1], w2_scales)
         deal_words(nc.vector, w_dealt[1], w_raw[1])
         w_raw.append(sb.tile([P, 2 * H], U8, name="w_raw2", tag="w_raw1", align_bytes=64))
         nc.sync.dma_start(out=w_raw[2][:].bitcast(I32), in_=w3_words[0].bitcast(I32))
+        load_scale_rows([nc.sync] * 4, ws_raw[2], w3_scales)
         gw = [sb.tile([P, HALF], U32, name="gw0", tag="gw0", align_bytes=64)]
         gs = [sb.tile([P, HALF], U8, name="gs0", align_bytes=64)]
         nc.vector.tensor_copy(gw[0][:], xw[:].indirect(offs_t[:, : HALF // 16]))
@@ -112,9 +115,12 @@ def tile_picked_delivmat_none_po_kernel(
             for t in range(PACK):
                 product(nc, y_ps[c][:, t, :], w_dealt[0], ws_dealt[0], t, gw[h][:, r * CH : (r + 1) * CH], gs[h][:, r * CH : (r + 1) * CH])
 
-        z = [sb.tile([P, CH, PACK], BF16, name="z%d" % c, tag="z%d" % c, align_bytes=64) for c in range(NCH)]
-        zc = [sb.tile([P, CH], U32, name="zc%d" % c, tag="zc%d" % c, align_bytes=64) for c in range(NCH)]
-        zs = [sb.tile([P, CH], U8, name="zs%d" % c, tag="zs%d" % c, align_bytes=64) for c in range(NCH)]
+        z = [sb.tile([P, CH, PACK], BF16, name="z%d" % c, align_bytes=64) for c in (0, 1)]
+        z.extend(stage.tile([P, CH, PACK], BF16, name="z%d" % c, align_bytes=64, offset=(c - 1) * 1024) for c in (2, 3))
+        z_codes = sb.tile([P, S], U32, name="z_codes", align_bytes=64)
+        z_scales = sb.tile([P, S], U8, name="z_scales", align_bytes=64)
+        zc = [z_codes[:, c * CH : (c + 1) * CH] for c in range(NCH)]
+        zs = [z_scales[:, c * CH : (c + 1) * CH] for c in range(NCH)]
         order = (2, 0, 1, 3)
         a_ends = [ps.tile([P, 2, HALF], F32, name="a_ends%d" % h, tag="hi%d" % h) for h in range(2)]
         a_mid = [ps.tile([P, 2, HALF], F32, name="a_mid%d" % i, tag="hi%d" % (2 + i)) for i in range(2)]
@@ -132,17 +138,16 @@ def tile_picked_delivmat_none_po_kernel(
             )
 
         def quantise(c):
-            nc.vector.quantize_mx(out=zc[c][:].bitcast(FP8X4), scales=zs[c][:], in_=z[c][:].rearrange("p j t -> p (j t)"))
+            nc.vector.quantize_mx(out=zc[c].bitcast(FP8X4), scales=zs[c], in_=z[c][:].rearrange("p j t -> p (j t)"))
 
         def second(t, c):
-            product(nc, a_ps[t][c // 2][:, c % 2 * CH : (c % 2 + 1) * CH], w_dealt[1], ws_dealt[1], t, zc[c][:], zs[c][:])
+            product(nc, a_ps[t][c // 2][:, c % 2 * CH : (c % 2 + 1) * CH], w_dealt[1], ws_dealt[1], t, zc[c], zs[c])
 
         for t in range(PACK):
             nc.scalar.activation(z[0][:, :, t], y_ps[0][:, t, :], ACT.Copy, scale=gain[:, t : t + 1])
         ws_dealt.append(sb.tile([P, H], U8, name="ws_dealt1", tag="gw0", align_bytes=64))
         scale(1)
         deal_scales(nc.vector, ws_dealt[1], ws_raw[1])
-        load_scale_rows([nc.sync] * 4, ws_raw[1], w3_scales)
         scale(2)
         quantise(1)
         quantise(0)
@@ -153,7 +158,6 @@ def tile_picked_delivmat_none_po_kernel(
         state = {
             order[0]: sb.tile([P, S], F32, name="state_a", tag="state_a"),
             order[1]: sb.tile([P, S], F32, name="state_b"),
-            order[2]: sb.tile([P, S], F32, name="state_c", tag="zs3", align_bytes=64),
         }
         hid = [sb.tile([P, S], F32, name="hid%d" % t, tag="hid%d" % t, align_bytes=64) for t in range(PACK)]
         msg = [sb.tile([P, V], F32, name="msg%d" % t) for t in range(PACK)]
@@ -193,27 +197,32 @@ def tile_picked_delivmat_none_po_kernel(
             for t in order[:2]:
                 fill(t, [c])
 
-        w_dealt.append(sb.tile([P, 2 * H], U8, name="w_dealt2", tag="z3", align_bytes=64))
+        w_dealt.append(stage.tile([P, 2 * H], U8, name="w_dealt2", align_bytes=64, offset=2560))
         deal_words(nc.vector, w_dealt[2], w_raw[2])
+        ws_dealt.append(stage.tile([P, H], U8, name="ws_dealt2", align_bytes=64, offset=2048))
+        deal_scales(nc.vector, ws_dealt[2], ws_raw[2])
 
         tanh_mid(0)
         tanh_mid(1)
         tanh_half(order[3], 0)
         tanh_half(order[3], 1)
         fetch(order[0])
-        ws_dealt.append(sb.tile([P, H], U8, name="ws_dealt2", tag="hid%d" % order[0], align_bytes=64))
-        deal_scales(nc.vector, ws_dealt[2], ws_raw[1])
         fetch(order[1])
         deliver(order[0])
         fetch(order[2])
         deliver(order[1])
+        state.setdefault(order[2], sb.tile([P, S], F32, name="state_c", tag="hid%d" % order[0], align_bytes=64))
         fill(order[2], range(NCH))
         fetch(order[3])
         deliver(order[2])
         weave(order[0], range(NCH))
         state.setdefault(order[3], sb.tile([P, S], F32, name="state_d", tag="state_a"))
-        fill(order[3], range(NCH))
+        fill(order[3], range(NCH - 1))
         weave(order[1], range(NCH))
+        fill(order[3], [NCH - 1])
+        idle_ps = ps.tile([P, S], F32, name="idle_ps", tag="lo%d" % (NCH - 1))
+        for t in range(3):
+            product(nc, idle_ps[:], w_dealt[2], ws_dealt[2], t, z_codes[:], z_scales[:])
         deliver(order[3])
         weave(order[2], range(NCH))
 

@@ -226,12 +226,10 @@ def tile_picked_delivmat_none_po_kernel(
         deliver(order[3])
         weave(order[2], range(NCH))
 
-        z2c = [sb.tile([P, CH], U32, name="z2c%d" % c, align_bytes=64) for c in range(NCH)]
-        z2s = [sb.tile([P, CH], U8, name="z2s%d" % c, align_bytes=64) for c in range(NCH)]
-        o_ps = [
-            [ps.tile([P, 2, CH], F32, name="o_ps%d_%d" % (c, u), tag=("lo%d", "hi%d")[u] % c) for u in range(2)] for c in range(NCH)
-        ]
-        o32 = [sb.tile([P, PACK, CH], F32, name="o32_%d" % c) for c in range(NCH)]
+        z2c = [sb.tile([P, HALF], U32, name="z2c%d" % h, align_bytes=64) for h in range(2)]
+        z2s = [sb.tile([P, HALF], U8, name="z2s%d" % h, align_bytes=64) for h in range(2)]
+        o_ps = [[ps.tile([P, HALF], F32, name="o_ps%d_%d" % (h, t), tag=("hi%d", "lo%d")[h] % t) for t in range(PACK)] for h in range(2)]
+        o32 = [sb.tile([P, PACK, HALF], F32, name="o32_%d" % h) for h in range(2)]
         o16 = [sb.tile([P, CH, PACK], BF16, name="o16_%d" % c, align_bytes=64) for c in range(NCH)]
         oc = sb.tile([P, S], U32, name="oc", align_bytes=64)
         osc = sb.tile([P, S], U8, name="osc", align_bytes=64)
@@ -242,31 +240,43 @@ def tile_picked_delivmat_none_po_kernel(
         def weave_last(c):
             nc.vector.tensor_scalar(z2[c][:, :, last], state[last][:, c * CH : (c + 1) * CH], gain[:, last : last + 1], None, MULT)
 
-        def third(c):
-            nc.vector.quantize_mx(out=z2c[c][:].bitcast(FP8X4), scales=z2s[c][:], in_=z2[c][:].rearrange("p j t -> p (j t)"))
-            for t in range(PACK):
-                product(nc, o_ps[c][t // 2][:, t % 2, :], w_dealt[2], ws_dealt[2], t, z2c[c][:], z2s[c][:])
+        def quantise_z2(c):
+            cols = slice(c % 2 * CH, (c % 2 + 1) * CH)
+            nc.vector.quantize_mx(
+                out=z2c[c // 2][:, cols].bitcast(FP8X4), scales=z2s[c // 2][:, cols], in_=z2[c][:].rearrange("p j t -> p (j t)")
+            )
+
+        def store_rows(h, planes):
+            nc.sync.dma_start(out=out_rows[:, planes, h * HALF : (h + 1) * HALF], in_=o32[h][:, planes, :])
 
         weave_last(0)
-        weave(last, [1, 3])
-        weave_last(2)
-        third(0)
-        third(1)
-        third(2)
-        third(3)
-        for c in range(NCH):
-            cols = slice(c * CH, (c + 1) * CH)
-            for u in range(2):
-                nc.scalar.copy(o32[c][:, 2 * u : 2 * u + 2, :], o_ps[c][u][:])
-            nc.sync.dma_start(out=out_rows[:, :, cols], in_=o32[c][:])
-            nc.vector.tensor_copy(
-                out=o16[c][:].rearrange("p (j i) t -> p j t i", i=4),
-                in_=o32[c][:].rearrange("p t (j i) -> p j t i", i=4),
-            )
-            nc.vector.quantize_mx(out=oc[:, cols].bitcast(FP8X4), scales=osc[:, cols], in_=o16[c][:].rearrange("p j t -> p (j t)"))
-            if c >= 2:
-                done = slice(0, 3 * CH) if c == 2 else cols
-                nc.sync.dma_start(out=out_words[:, done], in_=oc[:, done].bitcast(I32))
+        weave_last(1)
+        weave(last, [2, 3])
+        for h in range(2):
+            quantise_z2(2 * h)
+            quantise_z2(2 * h + 1)
+            for t in range(PACK):
+                product(nc, o_ps[h][t][:], w_dealt[2], ws_dealt[2], t, z2c[h][:], z2s[h][:])
+        for t in range(PACK):
+            if t % 2 == 0:
+                nc.scalar.copy(o32[0][:, t, :], o_ps[0][t][:])
+            else:
+                nc.vector.tensor_copy(o32[0][:, t, :], o_ps[0][t][:])
+            store_rows(0, slice(t, t + 1))
+        for t in range(PACK):
+            nc.scalar.copy(o32[1][:, t, :], o_ps[1][t][:])
+            if t % 2 == 1:
+                store_rows(1, slice(t - 1, t + 1))
+        for h in range(2):
+            for c in (2 * h, 2 * h + 1):
+                nc.vector.tensor_copy(
+                    out=o16[c][:].rearrange("p (j i) t -> p j t i", i=4),
+                    in_=o32[h][:, :, c % 2 * CH : (c % 2 + 1) * CH].rearrange("p t (j i) -> p j t i", i=4),
+                )
+            for c in (2 * h, 2 * h + 1):
+                cols = slice(c * CH, (c + 1) * CH)
+                nc.vector.quantize_mx(out=oc[:, cols].bitcast(FP8X4), scales=osc[:, cols], in_=o16[c][:].rearrange("p j t -> p (j t)"))
+            nc.sync.dma_start(out=out_words[:, h * HALF : (h + 1) * HALF], in_=oc[:, h * HALF : (h + 1) * HALF].bitcast(I32))
         for q in range(4):
             queue = nc.sync if q == 0 else nc.scalar
             queue.dma_start(out=out_2[0, 4 * q : 4 * q + 4, :].bitcast(I32), in_=osc[32 * q : 32 * q + 4, :].bitcast(I32))

@@ -217,12 +217,8 @@ def tile_picked_delivmat_none_po_kernel(
         deliver(order[2])
         weave(order[0], range(NCH))
         state.setdefault(order[3], sb.tile([P, S], F32, name="state_d", tag="state_a"))
-        fill(order[3], range(NCH - 1))
+        fill(order[3], range(NCH))
         weave(order[1], range(NCH))
-        fill(order[3], [NCH - 1])
-        idle_ps = ps.tile([P, S], F32, name="idle_ps", tag="lo%d" % (NCH - 1))
-        for t in range(3):
-            product(nc, idle_ps[:], w_dealt[2], ws_dealt[2], t, z_codes[:], z_scales[:])
         deliver(order[3])
         weave(order[2], range(NCH))
 

@@ -103,7 +103,7 @@ def tile_picked_delivmat_none_po_kernel(
         gs = [sb.tile([P, HALF], U8, name="gs0", align_bytes=64)]
         nc.vector.tensor_copy(gw[0][:], xw[:].indirect(offs_t[:, : HALF // 16]))
         nc.vector.tensor_copy(gs[0][:], xs[:].indirect(offs_t[:, : HALF // 16]))
-        deal_scales(nc.vector, ws_dealt[0], ws_raw[0])
+        deal_scales(nc.gpsimd, ws_dealt[0], ws_raw[0])
         gs.append(sb.tile([P, HALF], U8, name="gs1", tag="ws_raw0", align_bytes=64))
         nc.vector.tensor_copy(gs[1][:], xs[:].indirect(offs_t[:, HALF // 16 :]))
         gw.append(sb.tile([P, HALF], U32, name="gw1", tag="xs", align_bytes=64))
@@ -115,8 +115,8 @@ def tile_picked_delivmat_none_po_kernel(
             for t in range(PACK):
                 product(nc, y_ps[c][:, t, :], w_dealt[0], ws_dealt[0], t, gw[h][:, r * CH : (r + 1) * CH], gs[h][:, r * CH : (r + 1) * CH])
 
-        z = [sb.tile([P, CH, PACK], BF16, name="z%d" % c, align_bytes=64) for c in (0, 1)]
-        z.extend(stage.tile([P, CH, PACK], BF16, name="z%d" % c, align_bytes=64, offset=(c - 1) * 1024) for c in (2, 3))
+        z = [sb.tile([P, CH, PACK], BF16, name="z%d" % c, align_bytes=64) for c in range(NCH - 1)]
+        z.append(stage.tile([P, CH, PACK], BF16, name="z3", align_bytes=64, offset=2560))
         z_codes = sb.tile([P, S], U32, name="z_codes", align_bytes=64)
         z_scales = sb.tile([P, S], U8, name="z_scales", align_bytes=64)
         zc = [z_codes[:, c * CH : (c + 1) * CH] for c in range(NCH)]
@@ -145,9 +145,9 @@ def tile_picked_delivmat_none_po_kernel(
 
         for t in range(PACK):
             nc.scalar.activation(z[0][:, :, t], y_ps[0][:, t, :], ACT.Copy, scale=gain[:, t : t + 1])
-        ws_dealt.append(sb.tile([P, H], U8, name="ws_dealt1", tag="gw0", align_bytes=64))
+        ws_dealt.append(sb.tile([P, H], U8, name="ws_dealt1", align_bytes=64))
         scale(1)
-        deal_scales(nc.vector, ws_dealt[1], ws_raw[1])
+        deal_scales(nc.gpsimd, ws_dealt[1], ws_raw[1])
         scale(2)
         quantise(1)
         quantise(0)
@@ -197,9 +197,9 @@ def tile_picked_delivmat_none_po_kernel(
             for t in order[:2]:
                 fill(t, [c])
 
-        w_dealt.append(stage.tile([P, 2 * H], U8, name="w_dealt2", align_bytes=64, offset=2560))
+        w_dealt.append(stage.tile([P, 2 * H], U8, name="w_dealt2", align_bytes=64, offset=3072))
         deal_words(nc.vector, w_dealt[2], w_raw[2])
-        ws_dealt.append(stage.tile([P, H], U8, name="ws_dealt2", align_bytes=64, offset=2048))
+        ws_dealt.append(stage.tile([P, H], U8, name="ws_dealt2", align_bytes=64, offset=2560))
         deal_scales(nc.vector, ws_dealt[2], ws_raw[2])
 
         tanh_mid(0)
@@ -222,10 +222,12 @@ def tile_picked_delivmat_none_po_kernel(
         deliver(order[3])
         weave(order[2], range(NCH))
 
-        z2c = [sb.tile([P, HALF], U32, name="z2c%d" % h, align_bytes=64) for h in range(2)]
-        z2s = [sb.tile([P, HALF], U8, name="z2s%d" % h, align_bytes=64) for h in range(2)]
-        o_ps = [[ps.tile([P, HALF], F32, name="o_ps%d_%d" % (h, t), tag=("hi%d", "lo%d")[h] % t) for t in range(PACK)] for h in range(2)]
-        o32 = [sb.tile([P, PACK, HALF], F32, name="o32_%d" % h) for h in range(2)]
+        z2c = [sb.tile([P, CH], U32, name="z2c%d" % c, align_bytes=64) for c in range(NCH)]
+        z2s = [sb.tile([P, CH], U8, name="z2s%d" % c, align_bytes=64) for c in range(NCH)]
+        o_ps = [
+            [ps.tile([P, 2, CH], F32, name="o_ps%d_%d" % (c, u), tag=("lo%d", "hi%d")[u] % c) for u in range(2)] for c in range(NCH)
+        ]
+        o32 = [sb.tile([P, PACK, CH], F32, name="o32_%d" % c) for c in range(NCH)]
         o16 = [sb.tile([P, CH, PACK], BF16, name="o16_%d" % c, align_bytes=64) for c in range(NCH)]
         oc = sb.tile([P, S], U32, name="oc", align_bytes=64)
         osc = sb.tile([P, S], U8, name="osc", align_bytes=64)
@@ -236,43 +238,31 @@ def tile_picked_delivmat_none_po_kernel(
         def weave_last(c):
             nc.vector.tensor_scalar(z2[c][:, :, last], state[last][:, c * CH : (c + 1) * CH], gain[:, last : last + 1], None, MULT)
 
-        def quantise_z2(c):
-            cols = slice(c % 2 * CH, (c % 2 + 1) * CH)
-            nc.vector.quantize_mx(
-                out=z2c[c // 2][:, cols].bitcast(FP8X4), scales=z2s[c // 2][:, cols], in_=z2[c][:].rearrange("p j t -> p (j t)")
-            )
-
-        def store_rows(h, planes):
-            nc.sync.dma_start(out=out_rows[:, planes, h * HALF : (h + 1) * HALF], in_=o32[h][:, planes, :])
+        def third(c):
+            nc.vector.quantize_mx(out=z2c[c][:].bitcast(FP8X4), scales=z2s[c][:], in_=z2[c][:].rearrange("p j t -> p (j t)"))
+            for t in range(PACK):
+                product(nc, o_ps[c][t // 2][:, t % 2, :], w_dealt[2], ws_dealt[2], t, z2c[c][:], z2s[c][:])
 
         weave_last(0)
-        weave_last(1)
-        weave(last, [2, 3])
-        for h in range(2):
-            quantise_z2(2 * h)
-            quantise_z2(2 * h + 1)
-            for t in range(PACK):
-                product(nc, o_ps[h][t][:], w_dealt[2], ws_dealt[2], t, z2c[h][:], z2s[h][:])
-        for t in range(PACK):
-            if t % 2 == 0:
-                nc.scalar.copy(o32[0][:, t, :], o_ps[0][t][:])
-            else:
-                nc.vector.tensor_copy(o32[0][:, t, :], o_ps[0][t][:])
-            store_rows(0, slice(t, t + 1))
-        for t in range(PACK):
-            nc.scalar.copy(o32[1][:, t, :], o_ps[1][t][:])
-            if t % 2 == 1:
-                store_rows(1, slice(t - 1, t + 1))
-        for h in range(2):
-            for c in (2 * h, 2 * h + 1):
-                nc.vector.tensor_copy(
-                    out=o16[c][:].rearrange("p (j i) t -> p j t i", i=4),
-                    in_=o32[h][:, :, c % 2 * CH : (c % 2 + 1) * CH].rearrange("p t (j i) -> p j t i", i=4),
-                )
-            for c in (2 * h, 2 * h + 1):
-                cols = slice(c * CH, (c + 1) * CH)
-                nc.vector.quantize_mx(out=oc[:, cols].bitcast(FP8X4), scales=osc[:, cols], in_=o16[c][:].rearrange("p j t -> p (j t)"))
-            nc.sync.dma_start(out=out_words[:, h * HALF : (h + 1) * HALF], in_=oc[:, h * HALF : (h + 1) * HALF].bitcast(I32))
+        weave(last, [1, 3])
+        weave_last(2)
+        third(0)
+        third(1)
+        third(2)
+        third(3)
+        for c in range(NCH):
+            cols = slice(c * CH, (c + 1) * CH)
+            for u in range(2):
+                nc.scalar.copy(o32[c][:, 2 * u : 2 * u + 2, :], o_ps[c][u][:])
+            nc.sync.dma_start(out=out_rows[:, :, cols], in_=o32[c][:])
+            nc.vector.tensor_copy(
+                out=o16[c][:].rearrange("p (j i) t -> p j t i", i=4),
+                in_=o32[c][:].rearrange("p t (j i) -> p j t i", i=4),
+            )
+            nc.vector.quantize_mx(out=oc[:, cols].bitcast(FP8X4), scales=osc[:, cols], in_=o16[c][:].rearrange("p j t -> p (j t)"))
+            if c >= 2:
+                done = slice(0, 3 * CH) if c == 2 else cols
+                nc.sync.dma_start(out=out_words[:, done], in_=oc[:, done].bitcast(I32))
         for q in range(4):
             queue = nc.sync if q == 0 else nc.scalar
             queue.dma_start(out=out_2[0, 4 * q : 4 * q + 4, :].bitcast(I32), in_=osc[32 * q : 32 * q + 4, :].bitcast(I32))

@@ -83,8 +83,8 @@ def tile_picked_delivmat_none_po_kernel(
         nc.sync.dma_start(src_t[:], src)
         nc.sync.dma_start(dst_t[:], dst)
         nc.sync.dma_start(out=xw[:].bitcast(I32), in_=x_words[0].rearrange("p c r -> p (c r)").bitcast(I32))
-        load_scale_rows([nc.scalar] * 4, xs, x_scales)
         load_scale_rows([nc.scalar] * 3 + [nc.gpsimd], ws_raw[0], w1_scales)
+        load_scale_rows([nc.scalar] * 4, xs, x_scales)
 
         nc.gpsimd.dma_start(out=gain[:], in_=gn.rearrange("(p t) o -> p (t o)", t=PACK))
         warm = sb.tile([P, 1], F32, name="warm")
@@ -117,20 +117,21 @@ def tile_picked_delivmat_none_po_kernel(
 
         z = [sb.tile([P, CH, PACK], BF16, name="z%d" % c, align_bytes=64) for c in range(NCH - 1)]
         z.append(stage.tile([P, CH, PACK], BF16, name="z3", align_bytes=64, offset=2560))
-        z_codes = sb.tile([P, S], U32, name="z_codes", align_bytes=64)
+        z_codes = sb.tile([P, S], U32, name="z_codes", tag="z_codes", align_bytes=64)
         z_scales = sb.tile([P, S], U8, name="z_scales", align_bytes=64)
         zc = [z_codes[:, c * CH : (c + 1) * CH] for c in range(NCH)]
         zs = [z_scales[:, c * CH : (c + 1) * CH] for c in range(NCH)]
-        order = (2, 0, 1, 3)
-        a_ends = [ps.tile([P, 2, HALF], F32, name="a_ends%d" % h, tag="hi%d" % h) for h in range(2)]
-        a_mid = [ps.tile([P, 2, HALF], F32, name="a_mid%d" % i, tag="hi%d" % (2 + i)) for i in range(2)]
+        order = (1, 3, 0, 2)
+        banks = [ps.tile([P, 2, 2, CH], F32, name="a_ps%d" % i, tag="hi%d" % i) for i in range(PACK)]
         a_ps = {
-            order[0]: [a_ends[h][:, 0, :] for h in range(2)],
-            order[1]: [a_mid[0][:, h, :] for h in range(2)],
-            order[2]: [a_mid[1][:, h, :] for h in range(2)],
-            order[3]: [a_ends[h][:, 1, :] for h in range(2)],
+            order[0]: [banks[h][:, 0] for h in range(2)],
+            order[1]: [banks[2][:, h] for h in range(2)],
+            order[2]: [banks[3][:, h] for h in range(2)],
+            order[3]: [banks[h][:, 1] for h in range(2)],
         }
         gain_b = gain[:].unsqueeze(1).unsqueeze(3).to_broadcast([P, CH // 2, PACK, 2])
+        gain_rows = sb.tile([P, 2, V], F32, name="gain_rows")
+        nc.gpsimd.tensor_copy(gain_rows[:], gain[:, 0:PACK:2].unsqueeze(2).to_broadcast([P, 2, V]))
 
         def scale(c):
             nc.vector.tensor_tensor(
@@ -141,86 +142,91 @@ def tile_picked_delivmat_none_po_kernel(
             nc.vector.quantize_mx(out=zc[c].bitcast(FP8X4), scales=zs[c], in_=z[c][:].rearrange("p j t -> p (j t)"))
 
         def second(t, c):
-            product(nc, a_ps[t][c // 2][:, c % 2 * CH : (c % 2 + 1) * CH], w_dealt[1], ws_dealt[1], t, zc[c], zs[c])
+            product(nc, a_ps[t][c % 2][:, c // 2, :], w_dealt[1], ws_dealt[1], t, zc[c], zs[c])
 
-        for t in range(PACK):
-            nc.scalar.activation(z[0][:, :, t], y_ps[0][:, t, :], ACT.Copy, scale=gain[:, t : t + 1])
-        ws_dealt.append(sb.tile([P, H], U8, name="ws_dealt1", align_bytes=64))
-        scale(1)
-        deal_scales(nc.gpsimd, ws_dealt[1], ws_raw[1])
-        scale(2)
-        quantise(1)
-        quantise(0)
-        scale(3)
-        quantise(2)
-        quantise(3)
-
-        state = {
-            order[0]: sb.tile([P, S], F32, name="state_a", tag="state_a"),
-            order[1]: sb.tile([P, S], F32, name="state_b"),
-        }
         hid = [sb.tile([P, S], F32, name="hid%d" % t, tag="hid%d" % t, align_bytes=64) for t in range(PACK)]
         msg = [sb.tile([P, V], F32, name="msg%d" % t) for t in range(PACK)]
         z2 = [sb.tile([P, CH, PACK], BF16, name="z2_%d" % c, align_bytes=64) for c in range(NCH)]
+        state = {order[0]: sb.tile([P, S], F32, name="state_a")}
 
-        def fill(t, chunks):
-            for c in chunks:
-                nc.scalar.copy(state[t][:, c * CH : (c + 1) * CH], y_ps[c][:, t, :])
+        def fill(t):
+            for c in range(NCH):
+                if t % 2:
+                    nc.scalar.copy(state[t][:, c * CH : (c + 1) * CH], y_ps[c][:, t, :])
+                else:
+                    nc.scalar.activation(state[t][:, c * CH : (c + 1) * CH], y_ps[c][:, t, :], ACT.Copy, scale=gain[:, t : t + 1])
 
         def tanh_half(t, h):
-            nc.scalar.activation(hid[t][:, h * HALF : (h + 1) * HALF], a_ps[t][h], ACT.Tanh)
+            nc.scalar.activation(hid[t][:].rearrange("p (a h j) -> p h a j", a=2, h=2)[:, h], a_ps[t][h], ACT.Tanh)
 
-        def tanh_mid(i):
-            nc.scalar.activation(hid[order[1 + i]][:], a_mid[i][:].rearrange("p h j -> p (h j)"), ACT.Tanh)
+        def tanh_whole(d):
+            nc.scalar.activation(hid[order[d]][:].rearrange("p (a h j) -> p h a j", a=2, h=2), banks[1 + d][:], ACT.Tanh)
 
         def fetch(t):
             nc.vector.tensor_copy(msg[t][:], hid[t][:].indirect(src_t[:]))
 
         def deliver(t):
-            nc.vector.tensor_copy(state[t][:].indirect(dst_t[:]), msg[t][:])
+            if t % 2:
+                nc.vector.tensor_copy(state[t][:].indirect(dst_t[:]), msg[t][:])
+            else:
+                nc.vector.tensor_tensor(state[t][:].indirect(dst_t[:]), msg[t][:], gain_rows[:, t // 2, :], MULT)
 
-        def weave(t, chunks):
-            for c in chunks:
-                nc.scalar.activation(z2[c][:, :, t], state[t][:, c * CH : (c + 1) * CH], ACT.Copy, scale=gain[:, t : t + 1])
+        def join(t):
+            nc.scalar.activation(state[t - 1][:, S:], state[t][:], ACT.Copy, scale=gain[:, t : t + 1])
 
-        for c in (1, 0):
-            for t in (order[0], order[3], order[1], order[2]):
-                second(t, c)
-        for t in order[:3]:
-            for c in (2, 3):
-                second(t, c)
+        def weave(copy, t, c, lo=0, hi=CH):
+            copy(z2[c][:, lo:hi, t : t + 2], state[t][:].rearrange("p (u j) -> p j u", u=2)[:, c * CH + lo : c * CH + hi, :])
+
+        ws_dealt.append(sb.tile([P, H], U8, name="ws_dealt1", align_bytes=64))
+        scale(0)
+        for t in range(PACK):
+            nc.scalar.activation(z[1][:, :, t], y_ps[1][:, t, :], ACT.Copy, scale=gain[:, t : t + 1])
+        deal_scales(nc.gpsimd, ws_dealt[1], ws_raw[1])
+        quantise(0)
+        scale(2)
+        scale(3)
+        quantise(2)
+        quantise(1)
+        quantise(3)
+
+        for t in order:
+            second(t, 0)
+        fill(order[0])
+        for c in (2, 1, 3):
+            second(order[0], c)
         tanh_half(order[0], 0)
         tanh_half(order[0], 1)
-        for c in (2, 3):
-            second(order[3], c)
-        for c in range(NCH):
-            for t in order[:2]:
-                fill(t, [c])
+        for t in order[1:]:
+            for c in (2, 1, 3):
+                second(t, c)
+        tanh_whole(1)
 
         w_dealt.append(stage.tile([P, 2 * H], U8, name="w_dealt2", align_bytes=64, offset=3072))
         deal_words(nc.vector, w_dealt[2], w_raw[2])
         ws_dealt.append(stage.tile([P, H], U8, name="ws_dealt2", align_bytes=64, offset=2560))
         deal_scales(nc.vector, ws_dealt[2], ws_raw[2])
 
-        tanh_mid(0)
-        tanh_mid(1)
-        tanh_half(order[3], 0)
-        tanh_half(order[3], 1)
+        state.setdefault(order[1], sb.tile([P, S], F32, name="state_b", tag="z_codes", align_bytes=64))
+        fill(order[1])
+        tanh_whole(2)
+        for h in range(2):
+            tanh_half(order[3], h)
         fetch(order[0])
         fetch(order[1])
         deliver(order[0])
         fetch(order[2])
         deliver(order[1])
-        state.setdefault(order[2], sb.tile([P, S], F32, name="state_c", tag="hid%d" % order[0], align_bytes=64))
-        fill(order[2], range(NCH))
+        state.setdefault(order[2], sb.tile([P, 2 * S], F32, name="state_c", tag="hid%d" % order[0], align_bytes=64))
+        fill(order[2])
+        state.setdefault(order[3], sb.tile([P, 2 * S], F32, name="state_d", tag="hid%d" % order[1], align_bytes=64))
+        fill(order[3])
+        join(order[0])
         fetch(order[3])
         deliver(order[2])
-        weave(order[0], range(NCH))
-        state.setdefault(order[3], sb.tile([P, S], F32, name="state_d", tag="state_a"))
-        fill(order[3], range(NCH))
-        weave(order[1], range(NCH))
+        join(order[1])
         deliver(order[3])
-        weave(order[2], range(NCH))
+        for c in range(NCH - 1):
+            weave(nc.scalar.copy, order[2], c)
 
         z2c = [sb.tile([P, CH], U32, name="z2c%d" % c, align_bytes=64) for c in range(NCH)]
         z2s = [sb.tile([P, CH], U8, name="z2s%d" % c, align_bytes=64) for c in range(NCH)]
@@ -235,26 +241,26 @@ def tile_picked_delivmat_none_po_kernel(
         out_words = out_1[0].rearrange("p c r -> p (c r)").bitcast(I32)
         last = order[3]
 
-        def weave_last(c):
-            nc.vector.tensor_scalar(z2[c][:, :, last], state[last][:, c * CH : (c + 1) * CH], gain[:, last : last + 1], None, MULT)
-
         def third(c):
             nc.vector.quantize_mx(out=z2c[c][:].bitcast(FP8X4), scales=z2s[c][:], in_=z2[c][:].rearrange("p j t -> p (j t)"))
             for t in range(PACK):
                 product(nc, o_ps[c][t // 2][:, t % 2, :], w_dealt[2], ws_dealt[2], t, z2c[c][:], z2s[c][:])
 
-        weave_last(0)
-        weave(last, [1, 3])
-        weave_last(2)
-        third(0)
-        third(1)
-        third(2)
-        third(3)
+        weave(nc.vector.tensor_copy, last, 0, 0, CH // 2)
+        weave(nc.scalar.copy, last, 0, CH // 2, CH)
+        weave(nc.scalar.copy, order[2], NCH - 1)
+        for c in range(NCH):
+            if c + 1 < NCH:
+                weave(nc.vector.tensor_copy, last, c + 1)
+            third(c)
         for c in range(NCH):
             cols = slice(c * CH, (c + 1) * CH)
             for u in range(2):
                 nc.scalar.copy(o32[c][:, 2 * u : 2 * u + 2, :], o_ps[c][u][:])
-            nc.sync.dma_start(out=out_rows[:, :, cols], in_=o32[c][:])
+                if c == 0:
+                    nc.sync.dma_start(out=out_rows[:, 2 * u : 2 * u + 2, cols], in_=o32[c][:, 2 * u : 2 * u + 2, :])
+            if c > 0:
+                nc.sync.dma_start(out=out_rows[:, :, cols], in_=o32[c][:])
             nc.vector.tensor_copy(
                 out=o16[c][:].rearrange("p (j i) t -> p j t i", i=4),
                 in_=o32[c][:].rearrange("p t (j i) -> p j t i", i=4),

@@ -66,48 +66,49 @@ def tile_picked_delivmat_none_po_kernel(
         offs_t = sb.tile([P, S // 16], U16, name="offs_t")
         src_t = sb.tile([P, V // 16], U16, name="src_t")
         dst_t = sb.tile([P, V // 16], U16, name="dst_t")
-        xw = sb.tile([P, T], U32, name="xw", align_bytes=64)
+        xw = sb.tile([P, T], U32, name="xw", tag="xw", align_bytes=64)
         xs = sb.tile([P, T], U8, name="xs", tag="xs", align_bytes=64)
         gain = sb.tile([P, PACK], F32, name="gain")
-        w_raw = [stage.tile([P, 2 * H], U8, name="w_raw0", align_bytes=64, offset=896), sb.tile([P, 2 * H], U8, name="w_raw1", tag="w_raw1", align_bytes=64)]
+        w_raw = [stage.tile([P, 2 * H], U8, name="w_raw0", align_bytes=64, offset=448)]
         ws_raw = [sb.tile([P, H], U8, name="ws_raw0", tag="ws_raw0", align_bytes=64)]
-        w_dealt = [sb.tile([P, 2 * H], U8, name="w_dealt%d" % i, tag="w_dealt%d" % i, align_bytes=64) for i in range(2)]
+        w_dealt = [sb.tile([P, 2 * H], U8, name="w_dealt0", align_bytes=64)]
         ws_dealt = [sb.tile([P, H], U8, name="ws_dealt0", align_bytes=64)]
 
-        nc.vector.memset(xs[:].bitcast(I32), 0)
         nc.vector.memset(ws_raw[0][:].bitcast(I32), 0)
+        nc.vector.memset(xs[:].bitcast(I32), 0)
 
         nc.scalar.dma_start(out=w_raw[0][:].bitcast(I32), in_=w1_words[0].bitcast(I32))
         nc.sync.dma_start(offs_t[:], offs)
-        nc.scalar.dma_start(out=w_raw[1][:].bitcast(I32), in_=w2_words[0].bitcast(I32))
+        nc.scalar.dma_start(out=gain[:], in_=gn.rearrange("(p t) o -> p (t o)", t=PACK))
         nc.sync.dma_start(src_t[:], src)
         nc.sync.dma_start(dst_t[:], dst)
         nc.sync.dma_start(out=xw[:].bitcast(I32), in_=x_words[0].rearrange("p c r -> p (c r)").bitcast(I32))
         load_scale_rows([nc.scalar] * 3 + [nc.gpsimd], ws_raw[0], w1_scales)
         load_scale_rows([nc.scalar] * 4, xs, x_scales)
 
-        nc.gpsimd.dma_start(out=gain[:], in_=gn.rearrange("(p t) o -> p (t o)", t=PACK))
         warm = sb.tile([P, 1], F32, name="warm")
         nc.scalar.activation(warm[:], gain[:, 0:1], ACT.Tanh)
 
         deal_words(nc.vector, w_dealt[0], w_raw[0])
-        for i, offset in ((1, 1792), (2, 512)):
-            ws_raw.append(stage.tile([P, H], U8, name="ws_raw%d" % i, align_bytes=64, offset=offset))
+        w_raw.append(stage.tile([P, 2 * H], U8, name="w_raw1", align_bytes=64, offset=1024))
+        nc.sync.dma_start(out=w_raw[1][:].bitcast(I32), in_=w2_words[0].bitcast(I32))
+        for i in (1, 2):
+            ws_raw.append(stage.tile([P, H], U8, name="ws_raw%d" % i, align_bytes=64, offset=(i - 1) * H))
             nc.vector.memset(ws_raw[i][:].bitcast(I32), 0)
         load_scale_rows([nc.sync] * 4, ws_raw[1], w2_scales)
-        deal_words(nc.vector, w_dealt[1], w_raw[1])
-        w_raw.append(sb.tile([P, 2 * H], U8, name="w_raw2", tag="w_raw1", align_bytes=64))
-        nc.sync.dma_start(out=w_raw[2][:].bitcast(I32), in_=w3_words[0].bitcast(I32))
-        load_scale_rows([nc.sync] * 4, ws_raw[2], w3_scales)
-        gw = [sb.tile([P, HALF], U32, name="gw0", tag="gw0", align_bytes=64)]
-        gs = [sb.tile([P, HALF], U8, name="gs0", align_bytes=64)]
+        gw = [sb.tile([P, HALF], U32, name="gw0", align_bytes=64)]
+        gs = [sb.tile([P, HALF], U8, name="gs%d" % h, align_bytes=64) for h in range(2)]
         nc.vector.tensor_copy(gw[0][:], xw[:].indirect(offs_t[:, : HALF // 16]))
         nc.vector.tensor_copy(gs[0][:], xs[:].indirect(offs_t[:, : HALF // 16]))
         deal_scales(nc.gpsimd, ws_dealt[0], ws_raw[0])
-        gs.append(sb.tile([P, HALF], U8, name="gs1", tag="ws_raw0", align_bytes=64))
         nc.vector.tensor_copy(gs[1][:], xs[:].indirect(offs_t[:, HALF // 16 :]))
         gw.append(sb.tile([P, HALF], U32, name="gw1", tag="xs", align_bytes=64))
         nc.vector.tensor_copy(gw[1][:], xw[:].indirect(offs_t[:, HALF // 16 :]))
+        w_dealt.append(sb.tile([P, 2 * H], U8, name="w_dealt1", tag="ws_raw0", align_bytes=64))
+        deal_words(nc.gpsimd, w_dealt[1], w_raw[1])
+        w_raw.append(sb.tile([P, 2 * H], U8, name="w_raw2", tag="xw", align_bytes=64))
+        nc.sync.dma_start(out=w_raw[2][:].bitcast(I32), in_=w3_words[0].bitcast(I32))
+        load_scale_rows([nc.sync] * 4, ws_raw[2], w3_scales)
 
         y_ps = [ps.tile([P, PACK, CH], F32, name="y_ps%d" % c, tag="lo%d" % c) for c in range(NCH)]
         for c in range(NCH):
@@ -115,14 +116,12 @@ def tile_picked_delivmat_none_po_kernel(
             for t in range(PACK):
                 product(nc, y_ps[c][:, t, :], w_dealt[0], ws_dealt[0], t, gw[h][:, r * CH : (r + 1) * CH], gs[h][:, r * CH : (r + 1) * CH])
 
-        z = [sb.tile([P, CH, PACK], BF16, name="z%d" % c, align_bytes=64) for c in range(NCH - 1)]
-        z.append(stage.tile([P, CH, PACK], BF16, name="z3", align_bytes=64, offset=2560))
+        z = [sb.tile([P, HALF, PACK], BF16, name="z0", align_bytes=64), stage.tile([P, HALF, PACK], BF16, name="z1", align_bytes=64, offset=2560)]
         z_codes = sb.tile([P, S], U32, name="z_codes", tag="z_codes", align_bytes=64)
         z_scales = sb.tile([P, S], U8, name="z_scales", align_bytes=64)
-        zc = [z_codes[:, c * CH : (c + 1) * CH] for c in range(NCH)]
-        zs = [z_scales[:, c * CH : (c + 1) * CH] for c in range(NCH)]
+        z_part = [z[c // 2][:, c % 2 * CH : (c % 2 + 1) * CH, :] for c in range(NCH)]
         order = (1, 3, 0, 2)
-        banks = [ps.tile([P, 2, 2, CH], F32, name="a_ps%d" % i, tag="hi%d" % i) for i in range(PACK)]
+        banks = [ps.tile([P, 2, HALF], F32, name="a_ps%d" % i, tag="hi%d" % i) for i in range(PACK)]
         a_ps = {
             order[0]: [banks[h][:, 0] for h in range(2)],
             order[1]: [banks[2][:, h] for h in range(2)],
@@ -135,14 +134,19 @@ def tile_picked_delivmat_none_po_kernel(
 
         def scale(c):
             nc.vector.tensor_tensor(
-                z[c][:].rearrange("p (j i) t -> p j t i", i=2), y_ps[c][:].rearrange("p t (j i) -> p j t i", i=2), gain_b, MULT
+                z_part[c].rearrange("p (j i) t -> p j t i", i=2), y_ps[c][:].rearrange("p t (j i) -> p j t i", i=2), gain_b, MULT
             )
 
-        def quantise(c):
-            nc.vector.quantize_mx(out=zc[c].bitcast(FP8X4), scales=zs[c], in_=z[c][:].rearrange("p j t -> p (j t)"))
+        def quantise(h):
+            cols = slice(h * HALF, (h + 1) * HALF)
+            nc.vector.quantize_mx(out=z_codes[:, cols].bitcast(FP8X4), scales=z_scales[:, cols], in_=z[h][:].rearrange("p j t -> p (j t)"))
 
-        def second(t, c):
-            product(nc, a_ps[t][c % 2][:, c // 2, :], w_dealt[1], ws_dealt[1], t, zc[c], zs[c])
+        def second_half(t, h):
+            cols = slice(h * HALF, (h + 1) * HALF)
+            product(nc, a_ps[t][h], w_dealt[1], ws_dealt[1], t, z_codes[:, cols], z_scales[:, cols])
+
+        def second_whole(d):
+            product(nc, banks[1 + d][:].rearrange("p h j -> p (h j)"), w_dealt[1], ws_dealt[1], order[d], z_codes[:], z_scales[:])
 
         hid = [sb.tile([P, S], F32, name="hid%d" % t, tag="hid%d" % t, align_bytes=64) for t in range(PACK)]
         msg = [sb.tile([P, V], F32, name="msg%d" % t) for t in range(PACK)]
@@ -157,10 +161,10 @@ def tile_picked_delivmat_none_po_kernel(
                     nc.scalar.activation(state[t][:, c * CH : (c + 1) * CH], y_ps[c][:, t, :], ACT.Copy, scale=gain[:, t : t + 1])
 
         def tanh_half(t, h):
-            nc.scalar.activation(hid[t][:].rearrange("p (a h j) -> p h a j", a=2, h=2)[:, h], a_ps[t][h], ACT.Tanh)
+            nc.scalar.activation(hid[t][:, h * HALF : (h + 1) * HALF], a_ps[t][h], ACT.Tanh)
 
         def tanh_whole(d):
-            nc.scalar.activation(hid[order[d]][:].rearrange("p (a h j) -> p h a j", a=2, h=2), banks[1 + d][:], ACT.Tanh)
+            nc.scalar.activation(hid[order[d]][:], banks[1 + d][:].rearrange("p h j -> p (h j)"), ACT.Tanh)
 
         def fetch(t):
             nc.vector.tensor_copy(msg[t][:], hid[t][:].indirect(src_t[:]))
@@ -178,27 +182,23 @@ def tile_picked_delivmat_none_po_kernel(
             copy(z2[c][:, lo:hi, t : t + 2], state[t][:].rearrange("p (u j) -> p j u", u=2)[:, c * CH + lo : c * CH + hi, :])
 
         ws_dealt.append(sb.tile([P, H], U8, name="ws_dealt1", align_bytes=64))
-        scale(0)
         for t in range(PACK):
-            nc.scalar.activation(z[1][:, :, t], y_ps[1][:, t, :], ACT.Copy, scale=gain[:, t : t + 1])
+            nc.scalar.activation(z_part[0][:, :, t], y_ps[0][:, t, :], ACT.Copy, scale=gain[:, t : t + 1])
         deal_scales(nc.gpsimd, ws_dealt[1], ws_raw[1])
-        quantise(0)
-        scale(2)
-        scale(3)
-        quantise(2)
-        quantise(1)
-        quantise(3)
+        for c in range(1, NCH):
+            scale(c)
+        for h in range(2):
+            quantise(h)
 
-        for t in order:
-            second(t, 0)
         fill(order[0])
-        for c in (2, 1, 3):
-            second(order[0], c)
-        tanh_half(order[0], 0)
-        tanh_half(order[0], 1)
-        for t in order[1:]:
-            for c in (2, 1, 3):
-                second(t, c)
+        for h in range(2):
+            second_half(order[0], h)
+        for h in range(2):
+            tanh_half(order[0], h)
+        second_whole(1)
+        second_whole(2)
+        for h in range(2):
+            second_half(order[3], h)
         tanh_whole(1)
 
         w_dealt.append(stage.tile([P, 2 * H], U8, name="w_dealt2", align_bytes=64, offset=3072))

@@ -42,11 +42,12 @@ def deal_scales(engine, dealt, raw):
     )
 
 
-def product(nc, out, w_dealt, ws_dealt, t, codes, scales):
+def product(nc, out, w_dealt, ws_dealt, t, codes, scales, ts=None):
+    ts = t if ts is None else ts
     nc.tensor.matmul_mx(
         out=out,
         lhsT=w_dealt[:, 2 * P * t : 2 * P * (t + 1)].bitcast(FP4X4),
-        lhsT_scale=ws_dealt[:, P * t : P * (t + 1)],
+        lhsT_scale=ws_dealt[:, P * ts : P * (ts + 1)],
         rhs=codes.bitcast(FP8X4),
         rhs_scale=scales,
         start=True,
@@ -66,87 +67,78 @@ def tile_picked_delivmat_none_po_kernel(
         offs_t = sb.tile([P, S // 16], U16, name="offs_t")
         src_t = sb.tile([P, V // 16], U16, name="src_t")
         dst_t = sb.tile([P, V // 16], U16, name="dst_t")
-        xw = sb.tile([P, T], U32, name="xw", tag="xw", align_bytes=64)
+        xw = sb.tile([P, T], U32, name="xw", align_bytes=64)
         xs = sb.tile([P, T], U8, name="xs", tag="xs", align_bytes=64)
         gain = sb.tile([P, PACK], F32, name="gain")
-        w_raw = [stage.tile([P, 2 * H], U8, name="w_raw0", align_bytes=64, offset=448)]
+        w_raw = [stage.tile([P, 2 * H], U8, name="w_raw0", align_bytes=64, offset=448), sb.tile([P, 2 * H], U8, name="w_raw1", tag="w_raw1", align_bytes=64)]
         ws_raw = [sb.tile([P, H], U8, name="ws_raw0", tag="ws_raw0", align_bytes=64)]
-        w_dealt = [sb.tile([P, 2 * H], U8, name="w_dealt0", align_bytes=64)]
-        ws_dealt = [sb.tile([P, H], U8, name="ws_dealt0", align_bytes=64)]
+        w_dealt = [sb.tile([P, 2 * H], U8, name="w_dealt%d" % i, align_bytes=64) for i in range(2)]
+        w1_scales_dealt = [sb.tile([P, H // 2], U8, name="w1_scales_dealt%d" % u, align_bytes=64) for u in range(2)]
+        ws_dealt = [None]
 
-        nc.vector.memset(ws_raw[0][:].bitcast(I32), 0)
         nc.vector.memset(xs[:].bitcast(I32), 0)
+        nc.vector.memset(ws_raw[0][:].bitcast(I32), 0)
 
-        nc.scalar.dma_start(out=w_raw[0][:].bitcast(I32), in_=w1_words[0].bitcast(I32))
+        nc.sync.dma_start(out=w_raw[0][:].bitcast(I32), in_=w1_words[0].bitcast(I32))
         nc.sync.dma_start(offs_t[:], offs)
-        nc.scalar.dma_start(out=gain[:], in_=gn.rearrange("(p t) o -> p (t o)", t=PACK))
+        nc.sync.dma_start(out=w_raw[1][:].bitcast(I32), in_=w2_words[0].bitcast(I32))
+        load_scale_rows([nc.sync] * 4, xs, x_scales)
+        nc.sync.dma_start(out=xw[:].bitcast(I32), in_=x_words[0].rearrange("p c r -> p (c r)").bitcast(I32))
+        load_scale_rows([nc.sync] * 4, ws_raw[0], w1_scales)
         nc.sync.dma_start(src_t[:], src)
         nc.sync.dma_start(dst_t[:], dst)
-        nc.sync.dma_start(out=xw[:].bitcast(I32), in_=x_words[0].rearrange("p c r -> p (c r)").bitcast(I32))
-        load_scale_rows([nc.scalar] * 3 + [nc.gpsimd], ws_raw[0], w1_scales)
-        load_scale_rows([nc.scalar] * 4, xs, x_scales)
 
+        nc.gpsimd.dma_start(out=gain[:], in_=gn.rearrange("(p t) o -> p (t o)", t=PACK))
         warm = sb.tile([P, 1], F32, name="warm")
         nc.scalar.activation(warm[:], gain[:, 0:1], ACT.Tanh)
 
         deal_words(nc.vector, w_dealt[0], w_raw[0])
-        w_raw.append(stage.tile([P, 2 * H], U8, name="w_raw1", align_bytes=64, offset=1024))
-        nc.sync.dma_start(out=w_raw[1][:].bitcast(I32), in_=w2_words[0].bitcast(I32))
         for i in (1, 2):
             ws_raw.append(stage.tile([P, H], U8, name="ws_raw%d" % i, align_bytes=64, offset=(i - 1) * H))
             nc.vector.memset(ws_raw[i][:].bitcast(I32), 0)
         load_scale_rows([nc.sync] * 4, ws_raw[1], w2_scales)
-        gw = [sb.tile([P, HALF], U32, name="gw0", align_bytes=64)]
-        gs = [sb.tile([P, HALF], U8, name="gs%d" % h, align_bytes=64) for h in range(2)]
-        nc.vector.tensor_copy(gw[0][:], xw[:].indirect(offs_t[:, : HALF // 16]))
-        nc.vector.tensor_copy(gs[0][:], xs[:].indirect(offs_t[:, : HALF // 16]))
-        deal_scales(nc.gpsimd, ws_dealt[0], ws_raw[0])
-        nc.vector.tensor_copy(gs[1][:], xs[:].indirect(offs_t[:, HALF // 16 :]))
-        gw.append(sb.tile([P, HALF], U32, name="gw1", tag="xs", align_bytes=64))
-        nc.vector.tensor_copy(gw[1][:], xw[:].indirect(offs_t[:, HALF // 16 :]))
-        w_dealt.append(sb.tile([P, 2 * H], U8, name="w_dealt1", tag="ws_raw0", align_bytes=64))
-        deal_words(nc.gpsimd, w_dealt[1], w_raw[1])
-        w_raw.append(sb.tile([P, 2 * H], U8, name="w_raw2", tag="xw", align_bytes=64))
+        deal_words(nc.vector, w_dealt[1], w_raw[1])
+        gs = sb.tile([P, S], U8, name="gs", align_bytes=64)
+        nc.vector.tensor_copy(gs[:], xs[:].indirect(offs_t[:]))
+        w_raw.append(stage.tile([P, 2 * H], U8, name="w_raw2", align_bytes=64, offset=1024))
         nc.sync.dma_start(out=w_raw[2][:].bitcast(I32), in_=w3_words[0].bitcast(I32))
         load_scale_rows([nc.sync] * 4, ws_raw[2], w3_scales)
+        gw = [sb.tile([P, HALF], U32, name="gw0", tag="xs", align_bytes=64), sb.tile([P, HALF], U32, name="gw1", tag="w_raw1", align_bytes=64)]
+        for h in range(2):
+            nc.vector.tensor_copy(gw[h][:], xw[:].indirect(offs_t[:, h * HALF // 16 : (h + 1) * HALF // 16]))
+            nc.gpsimd.tensor_copy(
+                out=w1_scales_dealt[h][:].rearrange("p (t m) -> p t m", t=2),
+                in_=ws_raw[0][:].rearrange("p (m t) -> p t m", t=PACK)[:, 2 * h : 2 * h + 2],
+            )
 
         y_ps = [ps.tile([P, PACK, CH], F32, name="y_ps%d" % c, tag="lo%d" % c) for c in range(NCH)]
         for c in range(NCH):
             h, r = divmod(c, 2)
             for t in range(PACK):
-                product(nc, y_ps[c][:, t, :], w_dealt[0], ws_dealt[0], t, gw[h][:, r * CH : (r + 1) * CH], gs[h][:, r * CH : (r + 1) * CH])
+                product(nc, y_ps[c][:, t, :], w_dealt[0], w1_scales_dealt[t // 2], t, gw[h][:, r * CH : (r + 1) * CH], gs[:, c * CH : (c + 1) * CH], t % 2)
 
-        z = [sb.tile([P, HALF, PACK], BF16, name="z0", align_bytes=64), stage.tile([P, HALF, PACK], BF16, name="z1", align_bytes=64, offset=2560)]
+        spans = [slice(c * CH, (c + 1) * CH) for c in range(NCH)]
+        z = [sb.tile([P, CH, PACK], BF16, name="z%d" % c, align_bytes=64) for c in range(NCH - 1)]
+        z.append(stage.tile([P, CH, PACK], BF16, name="z3", align_bytes=64, offset=2560))
         z_codes = sb.tile([P, S], U32, name="z_codes", tag="z_codes", align_bytes=64)
-        z_scales = sb.tile([P, S], U8, name="z_scales", align_bytes=64)
-        z_part = [z[c // 2][:, c % 2 * CH : (c % 2 + 1) * CH, :] for c in range(NCH)]
+        z_scales = sb.tile([P, S], U8, name="z_scales", tag="z_scales", align_bytes=64)
         order = (1, 3, 0, 2)
-        banks = [ps.tile([P, 2, HALF], F32, name="a_ps%d" % i, tag="hi%d" % i) for i in range(PACK)]
-        a_ps = {
-            order[0]: [banks[h][:, 0] for h in range(2)],
-            order[1]: [banks[2][:, h] for h in range(2)],
-            order[2]: [banks[3][:, h] for h in range(2)],
-            order[3]: [banks[h][:, 1] for h in range(2)],
-        }
+        a_first = [ps.tile([P, CH], F32, name="a_first%d" % c, tag="hi%d" % c) for c in range(NCH)]
+        a_ps = {}
         gain_b = gain[:].unsqueeze(1).unsqueeze(3).to_broadcast([P, CH // 2, PACK, 2])
-        gain_rows = sb.tile([P, 2, V], F32, name="gain_rows")
+        gain_rows = sb.tile([P, 2, V], F32, name="gain_rows", tag="ws_raw0", align_bytes=64)
         nc.gpsimd.tensor_copy(gain_rows[:], gain[:, 0:PACK:2].unsqueeze(2).to_broadcast([P, 2, V]))
 
         def scale(c):
             nc.vector.tensor_tensor(
-                z_part[c].rearrange("p (j i) t -> p j t i", i=2), y_ps[c][:].rearrange("p t (j i) -> p j t i", i=2), gain_b, MULT
+                z[c][:].rearrange("p (j i) t -> p j t i", i=2), y_ps[c][:].rearrange("p t (j i) -> p j t i", i=2), gain_b, MULT
             )
 
-        def quantise(h):
-            cols = slice(h * HALF, (h + 1) * HALF)
-            nc.vector.quantize_mx(out=z_codes[:, cols].bitcast(FP8X4), scales=z_scales[:, cols], in_=z[h][:].rearrange("p j t -> p (j t)"))
+        def quantise(i):
+            nc.vector.quantize_mx(out=z_codes[:, spans[i]].bitcast(FP8X4), scales=z_scales[:, spans[i]], in_=z[i][:].rearrange("p j t -> p (j t)"))
 
-        def second_half(t, h):
-            cols = slice(h * HALF, (h + 1) * HALF)
-            product(nc, a_ps[t][h], w_dealt[1], ws_dealt[1], t, z_codes[:, cols], z_scales[:, cols])
-
-        def second_whole(d):
-            product(nc, banks[1 + d][:].rearrange("p h j -> p (h j)"), w_dealt[1], ws_dealt[1], order[d], z_codes[:], z_scales[:])
+        def second(out, t, cols):
+            product(nc, out, w_dealt[1], ws_dealt[1], t, z_codes[:, cols], z_scales[:, cols])
 
         hid = [sb.tile([P, S], F32, name="hid%d" % t, tag="hid%d" % t, align_bytes=64) for t in range(PACK)]
         msg = [sb.tile([P, V], F32, name="msg%d" % t) for t in range(PACK)]
@@ -160,11 +152,8 @@ def tile_picked_delivmat_none_po_kernel(
                 else:
                     nc.scalar.activation(state[t][:, c * CH : (c + 1) * CH], y_ps[c][:, t, :], ACT.Copy, scale=gain[:, t : t + 1])
 
-        def tanh_half(t, h):
-            nc.scalar.activation(hid[t][:, h * HALF : (h + 1) * HALF], a_ps[t][h], ACT.Tanh)
-
-        def tanh_whole(d):
-            nc.scalar.activation(hid[order[d]][:], banks[1 + d][:].rearrange("p h j -> p (h j)"), ACT.Tanh)
+        def tanh(t):
+            nc.scalar.activation(hid[t][:], a_ps[t][:], ACT.Tanh)
 
         def fetch(t):
             nc.vector.tensor_copy(msg[t][:], hid[t][:].indirect(src_t[:]))
@@ -182,35 +171,42 @@ def tile_picked_delivmat_none_po_kernel(
             copy(z2[c][:, lo:hi, t : t + 2], state[t][:].rearrange("p (u j) -> p j u", u=2)[:, c * CH + lo : c * CH + hi, :])
 
         ws_dealt.append(sb.tile([P, H], U8, name="ws_dealt1", align_bytes=64))
-        for t in range(PACK):
-            nc.scalar.activation(z_part[0][:, :, t], y_ps[0][:, t, :], ACT.Copy, scale=gain[:, t : t + 1])
         deal_scales(nc.gpsimd, ws_dealt[1], ws_raw[1])
-        for c in range(1, NCH):
-            scale(c)
-        for h in range(2):
-            quantise(h)
+        scale(0)
+        for t in range(PACK):
+            nc.scalar.activation(z[1][:, :, t], y_ps[1][:, t, :], ACT.Copy, scale=gain[:, t : t + 1])
+        quantise(0)
+        scale(2)
+        scale(3)
+        late = (2, 1, 3)
+        for c in late:
+            quantise(c)
 
+        second(a_first[0][:], order[0], spans[0])
+        nc.scalar.activation(hid[order[0]][:, spans[0]], a_first[0][:], ACT.Tanh)
         fill(order[0])
-        for h in range(2):
-            second_half(order[0], h)
-        for h in range(2):
-            tanh_half(order[0], h)
-        second_whole(1)
-        second_whole(2)
-        for h in range(2):
-            second_half(order[3], h)
-        tanh_whole(1)
+        a_ps.setdefault(order[1], ps.tile([P, S], F32, name="a_second", tag="hi0"))
+        second(a_ps[order[1]][:, spans[0]], order[1], spans[0])
+        for c in late:
+            second(a_first[c][:], order[0], spans[c])
+        for c in late:
+            second(a_ps[order[1]][:, spans[c]], order[1], spans[c])
+        for c in late:
+            nc.scalar.activation(hid[order[0]][:, spans[c]], a_first[c][:], ACT.Tanh)
+        tanh(order[1])
+        for d in (2, 3):
+            a_ps.setdefault(order[d], ps.tile([P, S], F32, name="a_late%d" % d, tag="hi%d" % late[d - 2]))
+            second(a_ps[order[d]][:], order[d], slice(0, S))
 
         w_dealt.append(stage.tile([P, 2 * H], U8, name="w_dealt2", align_bytes=64, offset=3072))
         deal_words(nc.vector, w_dealt[2], w_raw[2])
-        ws_dealt.append(stage.tile([P, H], U8, name="ws_dealt2", align_bytes=64, offset=2560))
-        deal_scales(nc.vector, ws_dealt[2], ws_raw[2])
+        ws_dealt.append(sb.tile([P, H], U8, name="ws_dealt2", tag="z_scales", align_bytes=64))
+        deal_scales(nc.gpsimd, ws_dealt[2], ws_raw[2])
 
         state.setdefault(order[1], sb.tile([P, S], F32, name="state_b", tag="z_codes", align_bytes=64))
         fill(order[1])
-        tanh_whole(2)
-        for h in range(2):
-            tanh_half(order[3], h)
+        tanh(order[2])
+        tanh(order[3])
         fetch(order[0])
         fetch(order[1])
         deliver(order[0])

@@ -103,9 +103,9 @@ def tile_picked_delivmat_none_po_kernel(
         w_raw.append(stage.tile([P, 2 * H], U8, name="w_raw2", align_bytes=64, offset=1024))
         nc.sync.dma_start(out=w_raw[2][:].bitcast(I32), in_=w3_words[0].bitcast(I32))
         load_scale_rows([nc.sync] * 4, ws_raw[2], w3_scales)
-        gw = [sb.tile([P, HALF], U32, name="gw0", tag="xs", align_bytes=64), sb.tile([P, HALF], U32, name="gw1", tag="w_raw1", align_bytes=64)]
+        gw = sb.tile([P, S], U32, name="gw", tag="xs", align_bytes=64)
         for h in range(2):
-            nc.vector.tensor_copy(gw[h][:], xw[:].indirect(offs_t[:, h * HALF // 16 : (h + 1) * HALF // 16]))
+            nc.vector.tensor_copy(gw[:, h * HALF : (h + 1) * HALF], xw[:].indirect(offs_t[:, h * HALF // 16 : (h + 1) * HALF // 16]))
             nc.gpsimd.tensor_copy(
                 out=w1_scales_dealt[h][:].rearrange("p (t m) -> p t m", t=2),
                 in_=ws_raw[0][:].rearrange("p (m t) -> p t m", t=PACK)[:, 2 * h : 2 * h + 2],
@@ -113,9 +113,8 @@ def tile_picked_delivmat_none_po_kernel(
 
         y_ps = [ps.tile([P, PACK, CH], F32, name="y_ps%d" % c, tag="lo%d" % c) for c in range(NCH)]
         for c in range(NCH):
-            h, r = divmod(c, 2)
             for t in range(PACK):
-                product(nc, y_ps[c][:, t, :], w_dealt[0], w1_scales_dealt[t // 2], t, gw[h][:, r * CH : (r + 1) * CH], gs[:, c * CH : (c + 1) * CH], t % 2)
+                product(nc, y_ps[c][:, t, :], w_dealt[0], w1_scales_dealt[t // 2], t, gw[:, c * CH : (c + 1) * CH], gs[:, c * CH : (c + 1) * CH], t % 2)
 
         spans = [slice(c * CH, (c + 1) * CH) for c in range(NCH)]
         z = [sb.tile([P, CH, PACK], BF16, name="z%d" % c, align_bytes=64) for c in range(NCH - 1)]
@@ -141,7 +140,7 @@ def tile_picked_delivmat_none_po_kernel(
             product(nc, out, w_dealt[1], ws_dealt[1], t, z_codes[:, cols], z_scales[:, cols])
 
         hid = [sb.tile([P, S], F32, name="hid%d" % t, tag="hid%d" % t, align_bytes=64) for t in range(PACK)]
-        msg = [sb.tile([P, V], F32, name="msg%d" % t) for t in range(PACK)]
+        msg = [sb.tile([P, V], F32, name="msg%d" % t, tag="msg%d" % t) for t in range(PACK)]
         z2 = [sb.tile([P, CH, PACK], BF16, name="z2_%d" % c, align_bytes=64) for c in range(NCH)]
         state = {order[0]: sb.tile([P, S], F32, name="state_a")}
 
@@ -214,13 +213,16 @@ def tile_picked_delivmat_none_po_kernel(
         deliver(order[1])
         state.setdefault(order[2], sb.tile([P, 2 * S], F32, name="state_c", tag="hid%d" % order[0], align_bytes=64))
         fill(order[2])
-        state.setdefault(order[3], sb.tile([P, 2 * S], F32, name="state_d", tag="hid%d" % order[1], align_bytes=64))
-        fill(order[3])
         join(order[0])
+        state.setdefault(order[3], sb.tile([P, 2 * S], F32, name="state_d", tag="msg%d" % order[1]))
+        join(order[1])
+        fill(order[3])
         fetch(order[3])
         deliver(order[2])
-        join(order[1])
         deliver(order[3])
+        warm_ps = ps.tile([P, S], F32, name="warm_ps", tag="lo%d" % (NCH - 1))
+        for t in range(3):
+            product(nc, warm_ps[:], w_dealt[0], w1_scales_dealt[t // 2], t, gw[:], gs[:], t % 2)
         for c in range(NCH - 1):
             weave(nc.scalar.copy, order[2], c)
 
@@ -252,7 +254,8 @@ def tile_picked_delivmat_none_po_kernel(
         for c in range(NCH):
             cols = slice(c * CH, (c + 1) * CH)
             for u in range(2):
-                nc.scalar.copy(o32[c][:, 2 * u : 2 * u + 2, :], o_ps[c][u][:])
+                copy = nc.vector.tensor_copy if (c, u) == (1, 0) else nc.scalar.copy
+                copy(o32[c][:, 2 * u : 2 * u + 2, :], o_ps[c][u][:])
                 if c == 0:
                     nc.sync.dma_start(out=out_rows[:, 2 * u : 2 * u + 2, cols], in_=o32[c][:, 2 * u : 2 * u + 2, :])
             if c > 0:
@@ -262,9 +265,7 @@ def tile_picked_delivmat_none_po_kernel(
                 in_=o32[c][:].rearrange("p t (j i) -> p j t i", i=4),
             )
             nc.vector.quantize_mx(out=oc[:, cols].bitcast(FP8X4), scales=osc[:, cols], in_=o16[c][:].rearrange("p j t -> p (j t)"))
-            if c >= 2:
-                done = slice(0, 3 * CH) if c == 2 else cols
-                nc.sync.dma_start(out=out_words[:, done], in_=oc[:, done].bitcast(I32))
+        nc.sync.dma_start(out=out_words, in_=oc[:].bitcast(I32))
         for q in range(4):
             queue = nc.sync if q == 0 else nc.scalar
             queue.dma_start(out=out_2[0, 4 * q : 4 * q + 4, :].bitcast(I32), in_=osc[32 * q : 32 * q + 4, :].bitcast(I32))

@@ -67,28 +67,29 @@ def tile_picked_delivmat_none_po_kernel(
         offs_t = sb.tile([P, S // 16], U16, name="offs_t")
         src_t = sb.tile([P, V // 16], U16, name="src_t")
         dst_t = sb.tile([P, V // 16], U16, name="dst_t")
-        xw = sb.tile([P, T], U32, name="xw", align_bytes=64)
+        xw = sb.tile([P, T], U32, name="xw", tag="xw", align_bytes=64)
         xs = sb.tile([P, T], U8, name="xs", tag="xs", align_bytes=64)
         gain = sb.tile([P, PACK], F32, name="gain")
         w_raw = [stage.tile([P, 2 * H], U8, name="w_raw0", align_bytes=64, offset=448), sb.tile([P, 2 * H], U8, name="w_raw1", tag="w_raw1", align_bytes=64)]
         ws_raw = [sb.tile([P, H], U8, name="ws_raw0", tag="ws_raw0", align_bytes=64)]
-        w_dealt = [sb.tile([P, 2 * H], U8, name="w_dealt%d" % i, align_bytes=64) for i in range(2)]
+        w_dealt = [sb.tile([P, 2 * H], U8, name="w_dealt0", align_bytes=64)]
         w1_scales_dealt = [sb.tile([P, H // 2], U8, name="w1_scales_dealt%d" % u, align_bytes=64) for u in range(2)]
         ws_dealt = [None]
 
-        nc.vector.memset(xs[:].bitcast(I32), 0)
+        nc.vector.memset(xs[:, : T // 2].bitcast(I32), 0)
+        nc.gpsimd.memset(xs[:, T // 2 :].bitcast(I32), 0)
         nc.vector.memset(ws_raw[0][:].bitcast(I32), 0)
 
-        nc.sync.dma_start(out=w_raw[0][:].bitcast(I32), in_=w1_words[0].bitcast(I32))
         nc.sync.dma_start(offs_t[:], offs)
-        nc.sync.dma_start(out=w_raw[1][:].bitcast(I32), in_=w2_words[0].bitcast(I32))
-        load_scale_rows([nc.sync] * 4, xs, x_scales)
-        nc.sync.dma_start(out=xw[:].bitcast(I32), in_=x_words[0].rearrange("p c r -> p (c r)").bitcast(I32))
-        load_scale_rows([nc.sync] * 4, ws_raw[0], w1_scales)
         nc.sync.dma_start(src_t[:], src)
+        nc.sync.dma_start(out=w_raw[0][:].bitcast(I32), in_=w1_words[0].bitcast(I32))
+        load_scale_rows([nc.sync] * 2 + [nc.scalar] * 2, xs, x_scales)
+        nc.sync.dma_start(out=xw[:].bitcast(I32), in_=x_words[0].rearrange("p c r -> p (c r)").bitcast(I32))
+        nc.gpsimd.dma_start(out=gain[:], in_=gn.rearrange("(p t) o -> p (t o)", t=PACK))
+        load_scale_rows([nc.sync] * 3 + [nc.gpsimd], ws_raw[0], w1_scales)
+        nc.sync.dma_start(out=w_raw[1][:].bitcast(I32), in_=w2_words[0].bitcast(I32))
         nc.sync.dma_start(dst_t[:], dst)
 
-        nc.gpsimd.dma_start(out=gain[:], in_=gn.rearrange("(p t) o -> p (t o)", t=PACK))
         warm = sb.tile([P, 1], F32, name="warm")
         nc.scalar.activation(warm[:], gain[:, 0:1], ACT.Tanh)
 
@@ -97,7 +98,6 @@ def tile_picked_delivmat_none_po_kernel(
             ws_raw.append(stage.tile([P, H], U8, name="ws_raw%d" % i, align_bytes=64, offset=(i - 1) * H))
             nc.vector.memset(ws_raw[i][:].bitcast(I32), 0)
         load_scale_rows([nc.sync] * 4, ws_raw[1], w2_scales)
-        deal_words(nc.vector, w_dealt[1], w_raw[1])
         gs = sb.tile([P, S], U8, name="gs", align_bytes=64)
         nc.vector.tensor_copy(gs[:], xs[:].indirect(offs_t[:]))
         w_raw.append(stage.tile([P, 2 * H], U8, name="w_raw2", align_bytes=64, offset=1024))
@@ -110,6 +110,8 @@ def tile_picked_delivmat_none_po_kernel(
                 out=w1_scales_dealt[h][:].rearrange("p (t m) -> p t m", t=2),
                 in_=ws_raw[0][:].rearrange("p (m t) -> p t m", t=PACK)[:, 2 * h : 2 * h + 2],
             )
+        w_dealt.append(sb.tile([P, 2 * H], U8, name="w_dealt1", tag="xw", align_bytes=64))
+        deal_words(nc.vector, w_dealt[1], w_raw[1])
 
         y_ps = [ps.tile([P, PACK, CH], F32, name="y_ps%d" % c, tag="lo%d" % c) for c in range(NCH)]
         for c in range(NCH):
@@ -247,8 +249,9 @@ def tile_picked_delivmat_none_po_kernel(
         weave(nc.vector.tensor_copy, last, 0, 0, CH // 2)
         weave(nc.scalar.copy, last, 0, CH // 2, CH)
         weave(nc.scalar.copy, order[2], NCH - 1)
+        weave(nc.scalar.copy, last, NCH - 1)
         for c in range(NCH):
-            if c + 1 < NCH:
+            if c + 2 < NCH:
                 weave(nc.vector.tensor_copy, last, c + 1)
             third(c)
         for c in range(NCH):

@@ -233,7 +233,8 @@ def tile_picked_delivmat_none_po_kernel(
         o_ps = [
             [ps.tile([P, 2, CH], F32, name="o_ps%d_%d" % (c, u), tag=("lo%d", "hi%d")[u] % c) for u in range(2)] for c in range(NCH)
         ]
-        o32 = [sb.tile([P, PACK, CH], F32, name="o32_%d" % c) for c in range(NCH)]
+        o_late = sb.tile([P, PACK, HALF], F32, name="o_late")
+        o32 = [sb.tile([P, PACK, CH], F32, name="o32_%d" % c)[:] for c in range(2)] + [o_late[:, :, :CH], o_late[:, :, CH:]]
         o16 = [sb.tile([P, CH, PACK], BF16, name="o16_%d" % c, align_bytes=64) for c in range(NCH)]
         oc = sb.tile([P, S], U32, name="oc", align_bytes=64)
         osc = sb.tile([P, S], U8, name="osc", align_bytes=64)
@@ -261,11 +262,13 @@ def tile_picked_delivmat_none_po_kernel(
                 copy(o32[c][:, 2 * u : 2 * u + 2, :], o_ps[c][u][:])
                 if c == 0:
                     nc.sync.dma_start(out=out_rows[:, 2 * u : 2 * u + 2, cols], in_=o32[c][:, 2 * u : 2 * u + 2, :])
-            if c > 0:
-                nc.sync.dma_start(out=out_rows[:, :, cols], in_=o32[c][:])
+                if c == NCH - 1:
+                    nc.sync.dma_start(out=out_rows[:, 2 * u : 2 * u + 2, HALF:], in_=o_late[:, 2 * u : 2 * u + 2, :])
+            if c == 1:
+                nc.sync.dma_start(out=out_rows[:, :, cols], in_=o32[c])
             nc.vector.tensor_copy(
                 out=o16[c][:].rearrange("p (j i) t -> p j t i", i=4),
-                in_=o32[c][:].rearrange("p t (j i) -> p j t i", i=4),
+                in_=o32[c].rearrange("p t (j i) -> p j t i", i=4),
             )
             nc.vector.quantize_mx(out=oc[:, cols].bitcast(FP8X4), scales=osc[:, cols], in_=o16[c][:].rearrange("p j t -> p (j t)"))
         nc.sync.dma_start(out=out_words, in_=oc[:].bitcast(I32))

@@ -80,18 +80,19 @@ def tile_picked_delivmat_none_po_kernel(
         nc.gpsimd.memset(xs[:, T // 2 :].bitcast(I32), 0)
         nc.vector.memset(ws_raw[0][:].bitcast(I32), 0)
 
-        nc.sync.dma_start(offs_t[:], offs)
-        nc.sync.dma_start(src_t[:], src)
         nc.sync.dma_start(out=w_raw[0][:].bitcast(I32), in_=w1_words[0].bitcast(I32))
+        nc.sync.dma_start(offs_t[:], offs)
         load_scale_rows([nc.sync] * 2 + [nc.scalar] * 2, xs, x_scales)
         nc.sync.dma_start(out=xw[:].bitcast(I32), in_=x_words[0].rearrange("p c r -> p (c r)").bitcast(I32))
-        nc.gpsimd.dma_start(out=gain[:], in_=gn.rearrange("(p t) o -> p (t o)", t=PACK))
-        load_scale_rows([nc.sync] * 3 + [nc.gpsimd], ws_raw[0], w1_scales)
+        load_scale_rows([nc.sync] * 4, ws_raw[0], w1_scales)
         nc.sync.dma_start(out=w_raw[1][:].bitcast(I32), in_=w2_words[0].bitcast(I32))
+        nc.sync.dma_start(out=gain[:], in_=gn.rearrange("(p t) o -> p (t o)", t=PACK))
+        nc.sync.dma_start(src_t[:], src)
         nc.sync.dma_start(dst_t[:], dst)
 
-        warm = sb.tile([P, 1], F32, name="warm")
-        nc.scalar.activation(warm[:], gain[:, 0:1], ACT.Tanh)
+        warm = sb.tile([P, 2], F32, name="warm")
+        nc.gpsimd.memset(warm[:, 0:1], 0.0)
+        nc.scalar.activation(warm[:, 1:2], warm[:, 0:1], ACT.Tanh)
 
         deal_words(nc.vector, w_dealt[0], w_raw[0])
         for i in (1, 2):

@@ -15,12 +15,15 @@ FP8X4 = mybir.dt.float8_e4m3fn_x4
 FP4X4 = mybir.dt.float4_e2m1fn_x4
 ACT = mybir.ActivationFunctionType
 MULT = mybir.AluOpType.mult
+ADD = mybir.AluOpType.add
 
 P = 128
 PACK = 4
 CH = 128
 NCH = S // CH
 HALF = 256
+PICKED = 8192
+FIRST = 12288
 
 
 def load_scale_rows(queues, plane, scales):
@@ -28,7 +31,7 @@ def load_scale_rows(queues, plane, scales):
         queue.dma_start(out=plane[32 * q : 32 * q + 4, :].bitcast(I32), in_=scales[0, 4 * q : 4 * q + 4, :].bitcast(I32))
 
 
-def deal_words(engine, dealt, raw):
+def deal_word_bytes(engine, dealt, raw):
     engine.tensor_copy(
         out=dealt[:].rearrange("p (t m b) -> p t m b", t=PACK, b=2),
         in_=raw[:].rearrange("p (m t b) -> p t m b", t=PACK, b=2),
@@ -67,25 +70,27 @@ def tile_picked_delivmat_none_po_kernel(
         offs_t = sb.tile([P, S // 16], U16, name="offs_t")
         src_t = sb.tile([P, V // 16], U16, name="src_t")
         dst_t = sb.tile([P, V // 16], U16, name="dst_t")
-        xw = sb.tile([P, T], U32, name="xw", tag="xw", align_bytes=64)
-        xs = sb.tile([P, T], U8, name="xs", tag="xs", align_bytes=64)
+        xw = sb.tile([P, T], U32, name="xw", align_bytes=64)
+        xs = stage.tile([P, T], U8, name="xs", align_bytes=64, offset=PICKED)
         gain = sb.tile([P, PACK], F32, name="gain")
-        w_raw = [stage.tile([P, 2 * H], U8, name="w_raw0", align_bytes=64, offset=448), sb.tile([P, 2 * H], U8, name="w_raw1", tag="w_raw1", align_bytes=64)]
-        ws_raw = [sb.tile([P, H], U8, name="ws_raw0", tag="ws_raw0", align_bytes=64)]
-        w_dealt = [sb.tile([P, 2 * H], U8, name="w_dealt0", align_bytes=64)]
-        w1_scales_dealt = [sb.tile([P, H // 2], U8, name="w1_scales_dealt%d" % u, align_bytes=64) for u in range(2)]
-        ws_dealt = [None]
+        w1_raw = stage.tile([P, 2 * H], U8, name="w1_raw", align_bytes=64, offset=448)
+        w2_raw = sb.tile([P, 2 * H], U8, name="w2_raw", align_bytes=64)
+        s1_raw = sb.tile([P, H], U8, name="s1_raw", tag="s1_raw", align_bytes=64)
+        w1 = sb.tile([P, 2 * H], U8, name="w1", align_bytes=64)
+        w2 = sb.tile([P, 2 * H], U8, name="w2", align_bytes=64)
+        s1 = [sb.tile([P, H // 2], U8, name="s1_%d" % u, align_bytes=64) for u in range(2)]
+        s2 = sb.tile([P, H], U8, name="s2", align_bytes=64)
 
         nc.vector.memset(xs[:, : T // 2].bitcast(I32), 0)
         nc.gpsimd.memset(xs[:, T // 2 :].bitcast(I32), 0)
-        nc.vector.memset(ws_raw[0][:].bitcast(I32), 0)
+        nc.vector.memset(s1_raw[:].bitcast(I32), 0)
 
-        nc.sync.dma_start(out=w_raw[0][:].bitcast(I32), in_=w1_words[0].bitcast(I32))
+        nc.sync.dma_start(out=w1_raw[:].bitcast(I32), in_=w1_words[0].bitcast(I32))
         nc.sync.dma_start(offs_t[:], offs)
         load_scale_rows([nc.sync] * 2 + [nc.scalar] * 2, xs, x_scales)
         nc.sync.dma_start(out=xw[:].bitcast(I32), in_=x_words[0].rearrange("p c r -> p (c r)").bitcast(I32))
-        load_scale_rows([nc.sync] * 4, ws_raw[0], w1_scales)
-        nc.sync.dma_start(out=w_raw[1][:].bitcast(I32), in_=w2_words[0].bitcast(I32))
+        load_scale_rows([nc.sync] * 4, s1_raw, w1_scales)
+        nc.sync.dma_start(out=w2_raw[:].bitcast(I32), in_=w2_words[0].bitcast(I32))
         nc.sync.dma_start(out=gain[:], in_=gn.rearrange("(p t) o -> p (t o)", t=PACK))
         nc.sync.dma_start(src_t[:], src)
         nc.sync.dma_start(dst_t[:], dst)
@@ -94,140 +99,137 @@ def tile_picked_delivmat_none_po_kernel(
         nc.gpsimd.memset(warm[:, 0:1], 0.0)
         nc.scalar.activation(warm[:, 1:2], warm[:, 0:1], ACT.Tanh)
 
-        deal_words(nc.vector, w_dealt[0], w_raw[0])
-        for i in (1, 2):
-            ws_raw.append(stage.tile([P, H], U8, name="ws_raw%d" % i, align_bytes=64, offset=(i - 1) * H))
-            nc.vector.memset(ws_raw[i][:].bitcast(I32), 0)
-        load_scale_rows([nc.sync] * 4, ws_raw[1], w2_scales)
+        deal_word_bytes(nc.vector, w1, w1_raw)
+        s2_raw = stage.tile([P, H], U8, name="s2_raw", align_bytes=64, offset=0)
+        s3_raw = stage.tile([P, H], U8, name="s3_raw", align_bytes=64, offset=H)
+        nc.vector.memset(s2_raw[:].bitcast(I32), 0)
+        nc.vector.memset(s3_raw[:].bitcast(I32), 0)
+        load_scale_rows([nc.sync] * 4, s2_raw, w2_scales)
         gs = sb.tile([P, S], U8, name="gs", align_bytes=64)
         nc.vector.tensor_copy(gs[:], xs[:].indirect(offs_t[:]))
-        w_raw.append(stage.tile([P, 2 * H], U8, name="w_raw2", align_bytes=64, offset=1024))
-        nc.sync.dma_start(out=w_raw[2][:].bitcast(I32), in_=w3_words[0].bitcast(I32))
-        load_scale_rows([nc.sync] * 4, ws_raw[2], w3_scales)
-        gw = sb.tile([P, S], U32, name="gw", tag="xs", align_bytes=64)
-        for h in range(2):
-            nc.vector.tensor_copy(gw[:, h * HALF : (h + 1) * HALF], xw[:].indirect(offs_t[:, h * HALF // 16 : (h + 1) * HALF // 16]))
+        w3_raw = stage.tile([P, 2 * H], U8, name="w3_raw", align_bytes=64, offset=1024)
+        nc.sync.dma_start(out=w3_raw[:].bitcast(I32), in_=w3_words[0].bitcast(I32))
+        load_scale_rows([nc.sync] * 4, s3_raw, w3_scales)
+        gw = []
+        for c in range(NCH):
+            gw.append(stage.tile([P, CH], U32, name="gw%d" % c, align_bytes=64, offset=PICKED + 4 * CH * (2 * (c % 2) + c // 2)))
+            nc.vector.tensor_copy(gw[c][:], xw[:].indirect(offs_t[:, c * CH // 16 : (c + 1) * CH // 16]))
+        for u in range(2):
             nc.gpsimd.tensor_copy(
-                out=w1_scales_dealt[h][:].rearrange("p (t m) -> p t m", t=2),
-                in_=ws_raw[0][:].rearrange("p (m t) -> p t m", t=PACK)[:, 2 * h : 2 * h + 2],
+                out=s1[u][:].rearrange("p (t m) -> p t m", t=2),
+                in_=s1_raw[:].rearrange("p (m t) -> p t m", t=PACK)[:, 2 * u : 2 * u + 2],
             )
-        w_dealt.append(sb.tile([P, 2 * H], U8, name="w_dealt1", tag="xw", align_bytes=64))
-        deal_words(nc.vector, w_dealt[1], w_raw[1])
+        nc.scalar.copy(
+            w2[:].bitcast(U16).rearrange("p (t m) -> p t m", t=PACK),
+            w2_raw[:].bitcast(U16).rearrange("p (m t) -> p t m", t=PACK),
+        )
+        gain_row = sb.tile([P, V], F32, name="gain_row", tag="s1_raw", align_bytes=64)
+        nc.gpsimd.tensor_copy(gain_row[:], gain[:, 2:3].to_broadcast([P, V]))
+        deal_scales(nc.gpsimd, s2, s2_raw)
 
+        spans = [slice(c * CH, (c + 1) * CH) for c in range(NCH)]
         y_ps = [ps.tile([P, PACK, CH], F32, name="y_ps%d" % c, tag="lo%d" % c) for c in range(NCH)]
         for c in range(NCH):
             for t in range(PACK):
-                product(nc, y_ps[c][:, t, :], w_dealt[0], w1_scales_dealt[t // 2], t, gw[:, c * CH : (c + 1) * CH], gs[:, c * CH : (c + 1) * CH], t % 2)
+                product(nc, y_ps[c][:, t, :], w1, s1[t // 2], t, gw[c][:], gs[:, spans[c]], t % 2)
 
-        spans = [slice(c * CH, (c + 1) * CH) for c in range(NCH)]
-        z = [sb.tile([P, CH, PACK], BF16, name="z%d" % c, align_bytes=64) for c in range(NCH - 1)]
-        z.append(stage.tile([P, CH, PACK], BF16, name="z3", align_bytes=64, offset=2560))
-        z_codes = sb.tile([P, S], U32, name="z_codes", tag="z_codes", align_bytes=64)
+        z_low = sb.tile([P, HALF, PACK], BF16, name="z_low", align_bytes=64)
+        z = [z_low[:, :CH, :], z_low[:, CH:, :], sb.tile([P, CH, PACK], BF16, name="z2", align_bytes=64)[:]]
+        z.append(stage.tile([P, CH, PACK], BF16, name="z3", align_bytes=64, offset=3584)[:])
+        z_codes = [stage.tile([P, HALF], U32, name="z_codes%d" % h, align_bytes=64, offset=PICKED + 4 * HALF * h) for h in range(2)]
         z_scales = sb.tile([P, S], U8, name="z_scales", tag="z_scales", align_bytes=64)
-        order = (1, 3, 0, 2)
-        a_first = [ps.tile([P, CH], F32, name="a_first%d" % c, tag="hi%d" % c) for c in range(NCH)]
-        a_ps = {}
         gain_b = gain[:].unsqueeze(1).unsqueeze(3).to_broadcast([P, CH // 2, PACK, 2])
-        gain_rows = sb.tile([P, 2, V], F32, name="gain_rows", tag="ws_raw0", align_bytes=64)
-        nc.gpsimd.tensor_copy(gain_rows[:], gain[:, 0:PACK:2].unsqueeze(2).to_broadcast([P, 2, V]))
+        hid = {t: sb.tile([P, S], F32, name="hid%d" % t, align_bytes=64) for t in (0, 2, 3)}
+        hid.setdefault(1, stage.tile([P, S], F32, name="hid1", align_bytes=64, offset=FIRST))
+        msg = [sb.tile([P, V], F32, name="msg%d" % t) for t in range(PACK)]
+        z2 = [sb.tile([P, CH, PACK], BF16, name="z2_%d" % c, align_bytes=64) for c in range(NCH)]
+        state = {t: sb.tile([P, S], F32, name="state%d" % t) for t in (1, 3, 0)}
+        low_pair = sb.tile([P, 2 * S], F32, name="low_pair")
 
         def scale(c):
             nc.vector.tensor_tensor(
-                z[c][:].rearrange("p (j i) t -> p j t i", i=2), y_ps[c][:].rearrange("p t (j i) -> p j t i", i=2), gain_b, MULT
+                z[c].rearrange("p (j i) t -> p j t i", i=2), y_ps[c][:].rearrange("p t (j i) -> p j t i", i=2), gain_b, MULT
             )
 
-        def quantise(i):
-            nc.vector.quantize_mx(out=z_codes[:, spans[i]].bitcast(FP8X4), scales=z_scales[:, spans[i]], in_=z[i][:].rearrange("p j t -> p (j t)"))
+        def codes_of(cols):
+            return z_codes[cols.start // HALF][:, cols.start % HALF : cols.start % HALF + cols.stop - cols.start]
+
+        def quantise(values, cols):
+            nc.vector.quantize_mx(out=codes_of(cols).bitcast(FP8X4), scales=z_scales[:, cols], in_=values.rearrange("p j t -> p (j t)"))
 
         def second(out, t, cols):
-            product(nc, out, w_dealt[1], ws_dealt[1], t, z_codes[:, cols], z_scales[:, cols])
+            product(nc, out, w2, s2, t, codes_of(cols), z_scales[:, cols])
 
-        hid = [sb.tile([P, S], F32, name="hid%d" % t, tag="hid%d" % t, align_bytes=64) for t in range(PACK)]
-        msg = [sb.tile([P, V], F32, name="msg%d" % t, tag="msg%d" % t) for t in range(PACK)]
-        z2 = [sb.tile([P, CH, PACK], BF16, name="z2_%d" % c, align_bytes=64) for c in range(NCH)]
-        state = {order[0]: sb.tile([P, S], F32, name="state_a")}
-
-        def fill(t):
-            for c in range(NCH):
-                if t % 2:
-                    nc.scalar.copy(state[t][:, c * CH : (c + 1) * CH], y_ps[c][:, t, :])
-                else:
-                    nc.scalar.activation(state[t][:, c * CH : (c + 1) * CH], y_ps[c][:, t, :], ACT.Copy, scale=gain[:, t : t + 1])
-
-        def tanh(t):
-            nc.scalar.activation(hid[t][:], a_ps[t][:], ACT.Tanh)
+        def fill(t, c):
+            if t != 2:
+                nc.scalar.copy(state[t][:, spans[c]], y_ps[c][:, t, :])
+            else:
+                nc.scalar.activation(state[t][:, spans[c]], y_ps[c][:, t, :], ACT.Copy, scale=gain[:, t : t + 1])
 
         def fetch(t):
-            nc.vector.tensor_copy(msg[t][:], hid[t][:].indirect(src_t[:]))
+            nc.scalar.activation(msg[t][:], hid[t][:].indirect(src_t[:]), ACT.Copy)
 
         def deliver(t):
-            if t % 2:
+            if t != 2:
                 nc.vector.tensor_copy(state[t][:].indirect(dst_t[:]), msg[t][:])
             else:
-                nc.vector.tensor_tensor(state[t][:].indirect(dst_t[:]), msg[t][:], gain_rows[:, t // 2, :], MULT)
+                nc.vector.tensor_tensor(state[t][:].indirect(dst_t[:]), msg[t][:], gain_row[:], MULT)
 
-        def join(t):
-            nc.scalar.activation(state[t - 1][:, S:], state[t][:], ACT.Copy, scale=gain[:, t : t + 1])
+        def join(pair, t):
+            nc.gpsimd.tensor_scalar(pair[:, S:], state[t][:], gain[:, t : t + 1], 0.0, MULT, ADD)
 
         def weave(copy, t, c, lo=0, hi=CH):
-            copy(z2[c][:, lo:hi, t : t + 2], state[t][:].rearrange("p (u j) -> p j u", u=2)[:, c * CH + lo : c * CH + hi, :])
+            copy(z2[c][:, lo:hi, t : t + 2], (state[2] if t else low_pair)[:].rearrange("p (u j) -> p j u", u=2)[:, c * CH + lo : c * CH + hi, :])
 
-        ws_dealt.append(sb.tile([P, H], U8, name="ws_dealt1", align_bytes=64))
-        deal_scales(nc.gpsimd, ws_dealt[1], ws_raw[1])
-        scale(0)
-        for t in range(PACK):
-            nc.scalar.activation(z[1][:, :, t], y_ps[1][:, t, :], ACT.Copy, scale=gain[:, t : t + 1])
-        quantise(0)
-        scale(2)
-        scale(3)
-        late = (2, 1, 3)
-        for c in late:
-            quantise(c)
+        pieces = [slice(0, HALF), spans[2], spans[3]]
+        a_first = [ps.tile([P, pieces[i].stop - pieces[i].start], F32, name="a_first%d" % i, tag="hi%d" % i) for i in range(3)]
 
-        second(a_first[0][:], order[0], spans[0])
-        nc.scalar.activation(hid[order[0]][:, spans[0]], a_first[0][:], ACT.Tanh)
-        fill(order[0])
-        a_ps.setdefault(order[1], ps.tile([P, S], F32, name="a_second", tag="hi0"))
-        second(a_ps[order[1]][:, spans[0]], order[1], spans[0])
-        for c in late:
-            second(a_first[c][:], order[0], spans[c])
-        for c in late:
-            second(a_ps[order[1]][:, spans[c]], order[1], spans[c])
-        for c in late:
-            nc.scalar.activation(hid[order[0]][:, spans[c]], a_first[c][:], ACT.Tanh)
-        tanh(order[1])
-        for d in (2, 3):
-            a_ps.setdefault(order[d], ps.tile([P, S], F32, name="a_late%d" % d, tag="hi%d" % late[d - 2]))
-            second(a_ps[order[d]][:], order[d], slice(0, S))
+        def first_messages(i):
+            second(a_first[i][:], 1, pieces[i])
+            nc.scalar.activation(hid[1][:, pieces[i]], a_first[i][:], ACT.Tanh)
 
-        w_dealt.append(stage.tile([P, 2 * H], U8, name="w_dealt2", align_bytes=64, offset=3072))
-        deal_words(nc.vector, w_dealt[2], w_raw[2])
-        ws_dealt.append(sb.tile([P, H], U8, name="ws_dealt2", tag="z_scales", align_bytes=64))
-        deal_scales(nc.gpsimd, ws_dealt[2], ws_raw[2])
+        for c in range(NCH):
+            scale(c)
+            if c >= 2:
+                quantise((z_low[:], z[2])[c - 2], pieces[c - 2])
+                first_messages(c - 2)
+            fill(1, c)
+            if c < NCH - 1:
+                fill(3, c)
+                fill(0, c)
+        quantise(z[3], pieces[2])
+        first_messages(2)
+        a_ps = {}
 
-        state.setdefault(order[1], sb.tile([P, S], F32, name="state_b", tag="z_codes", align_bytes=64))
-        fill(order[1])
-        tanh(order[2])
-        tanh(order[3])
-        fetch(order[0])
-        fetch(order[1])
-        deliver(order[0])
-        fetch(order[2])
-        deliver(order[1])
-        state.setdefault(order[2], sb.tile([P, 2 * S], F32, name="state_c", tag="hid%d" % order[0], align_bytes=64))
-        fill(order[2])
-        join(order[0])
-        state.setdefault(order[3], sb.tile([P, 2 * S], F32, name="state_d", tag="msg%d" % order[1]))
-        join(order[1])
-        fill(order[3])
-        fetch(order[3])
-        deliver(order[2])
-        deliver(order[3])
-        warm_ps = ps.tile([P, S], F32, name="warm_ps", tag="lo%d" % (NCH - 1))
-        for t in range(3):
-            product(nc, warm_ps[:], w_dealt[0], w1_scales_dealt[t // 2], t, gw[:], gs[:], t % 2)
-        for c in range(NCH - 1):
-            weave(nc.scalar.copy, order[2], c)
+        def messages(t, chunks):
+            a_ps.setdefault(t, ps.tile([P, S], F32, name="a_ps%d" % t, tag="hi%d" % {3: 3, 0: 0, 2: 1}[t]))
+            for h in (1, 0):
+                second(a_ps[t][:, h * HALF : (h + 1) * HALF], t, slice(h * HALF, (h + 1) * HALF))
+            nc.scalar.activation(hid[t][:], a_ps[t][:], ACT.Tanh)
+            fetch(t)
+            for c in chunks:
+                fill(t, c)
+
+        w3 = stage.tile([P, 2 * H], U8, name="w3", align_bytes=64, offset=3072)
+        deal_word_bytes(nc.vector, w3, w3_raw)
+        s3 = stage.tile([P, H], U8, name="s3", align_bytes=64, offset=4096)
+        deal_scales(nc.vector, s3, s3_raw)
+        nc.vector.tensor_copy(msg[1][:], hid[1][:].indirect(src_t[:]))
+        deliver(1)
+        join(low_pair, 1)
+        state.setdefault(2, stage.tile([P, 2 * S], F32, name="state2", align_bytes=64, offset=FIRST + H))
+        messages(3, [])
+        fill(2, NCH - 1)
+        fill(3, NCH - 1)
+        deliver(3)
+        join(state[2], 3)
+        messages(0, [NCH - 1])
+        deliver(0)
+        messages(2, range(NCH - 1))
+        deliver(2)
+        nc.scalar.activation(low_pair[:, :S], state[0][:], ACT.Copy, scale=gain[:, 0:1])
+        for c in range(NCH):
+            weave(nc.scalar.copy, 0, c)
 
         z2c = [sb.tile([P, CH], U32, name="z2c%d" % c, align_bytes=64) for c in range(NCH)]
         z2s = [sb.tile([P, CH], U8, name="z2s%d" % c, align_bytes=64) for c in range(NCH)]
@@ -241,23 +243,21 @@ def tile_picked_delivmat_none_po_kernel(
         osc = sb.tile([P, S], U8, name="osc", align_bytes=64)
         out_rows = out_0.rearrange("(p t) j -> p t j", t=PACK)
         out_words = out_1[0].rearrange("p c r -> p (c r)").bitcast(I32)
-        last = order[3]
+        last = 2
 
         def third(c):
             nc.vector.quantize_mx(out=z2c[c][:].bitcast(FP8X4), scales=z2s[c][:], in_=z2[c][:].rearrange("p j t -> p (j t)"))
             for t in range(PACK):
-                product(nc, o_ps[c][t // 2][:, t % 2, :], w_dealt[2], ws_dealt[2], t, z2c[c][:], z2s[c][:])
+                product(nc, o_ps[c][t // 2][:, t % 2, :], w3, s3, t, z2c[c][:], z2s[c][:])
 
-        weave(nc.vector.tensor_copy, last, 0, 0, CH // 2)
-        weave(nc.scalar.copy, last, 0, CH // 2, CH)
-        weave(nc.scalar.copy, order[2], NCH - 1)
+        weave(nc.vector.tensor_copy, last, 0)
         weave(nc.scalar.copy, last, NCH - 1)
         for c in range(NCH):
             if c + 2 < NCH:
                 weave(nc.vector.tensor_copy, last, c + 1)
             third(c)
         for c in range(NCH):
-            cols = slice(c * CH, (c + 1) * CH)
+            cols = spans[c]
             for u in range(2):
                 copy = nc.vector.tensor_copy if (c, u) == (1, 0) else nc.scalar.copy
                 copy(o32[c][:, 2 * u : 2 * u + 2, :], o_ps[c][u][:])

@@ -123,8 +123,8 @@ def tile_picked_delivmat_none_po_kernel(
             w2[:].bitcast(U16).rearrange("p (t m) -> p t m", t=PACK),
             w2_raw[:].bitcast(U16).rearrange("p (m t) -> p t m", t=PACK),
         )
-        gain_row = sb.tile([P, V], F32, name="gain_row", tag="s1_raw", align_bytes=64)
-        nc.gpsimd.tensor_copy(gain_row[:], gain[:, 2:3].to_broadcast([P, V]))
+        gain_row = sb.tile([P, V], F32, name="gain_row")
+        nc.scalar.copy(gain_row[:], gain[:, 2:3].to_broadcast([P, V]))
         deal_scales(nc.gpsimd, s2, s2_raw)
 
         spans = [slice(c * CH, (c + 1) * CH) for c in range(NCH)]
@@ -175,8 +175,8 @@ def tile_picked_delivmat_none_po_kernel(
             else:
                 nc.vector.tensor_tensor(state[t][:].indirect(dst_t[:]), msg[t][:], gain_row[:], MULT)
 
-        def join(pair, t):
-            nc.gpsimd.tensor_scalar(pair[:, S:], state[t][:], gain[:, t : t + 1], 0.0, MULT, ADD)
+        def join(pair, t, factor):
+            nc.gpsimd.tensor_scalar(pair[:, S:], state[t][:], factor, 0.0, MULT, ADD)
 
         def weave(copy, t, c, lo=0, hi=CH):
             copy(z2[c][:, lo:hi, t : t + 2], (state[2] if t else low_pair)[:].rearrange("p (u j) -> p j u", u=2)[:, c * CH + lo : c * CH + hi, :])
@@ -212,17 +212,19 @@ def tile_picked_delivmat_none_po_kernel(
 
         w3 = stage.tile([P, 2 * H], U8, name="w3", align_bytes=64, offset=3072)
         deal_word_bytes(nc.vector, w3, w3_raw)
-        s3 = stage.tile([P, H], U8, name="s3", align_bytes=64, offset=4096)
-        deal_scales(nc.vector, s3, s3_raw)
         nc.vector.tensor_copy(msg[1][:], hid[1][:].indirect(src_t[:]))
         deliver(1)
-        join(low_pair, 1)
+        s3 = stage.tile([P, H], U8, name="s3", align_bytes=64, offset=FIRST)
+        deal_scales(nc.gpsimd, s3, s3_raw)
+        join(low_pair, 1, gain[:, 1:2])
         state.setdefault(2, stage.tile([P, 2 * S], F32, name="state2", align_bytes=64, offset=FIRST + H))
         messages(3, [])
         fill(2, NCH - 1)
         fill(3, NCH - 1)
         deliver(3)
-        join(state[2], 3)
+        gain_last = stage.tile([P, 1], F32, name="gain_last", align_bytes=64, offset=H)
+        nc.gpsimd.tensor_copy(gain_last[:], gain[:, 3:4])
+        join(state[2], 3, gain_last[:])
         messages(0, [NCH - 1])
         deliver(0)
         messages(2, range(NCH - 1))

@@ -24,6 +24,7 @@ NCH = S // CH
 HALF = 256
 PICKED = 8192
 FIRST = 12288
+LAST = 20480
 
 
 def load_scale_rows(queues, plane, scales):
@@ -141,8 +142,11 @@ def tile_picked_delivmat_none_po_kernel(
         gain_b = gain[:].unsqueeze(1).unsqueeze(3).to_broadcast([P, CH // 2, PACK, 2])
         hid = {t: sb.tile([P, S], F32, name="hid%d" % t, align_bytes=64) for t in (0, 2, 3)}
         hid.setdefault(1, stage.tile([P, S], F32, name="hid1", align_bytes=64, offset=FIRST))
-        msg = [sb.tile([P, V], F32, name="msg%d" % t) for t in range(PACK)]
-        z2 = [sb.tile([P, CH, PACK], BF16, name="z2_%d" % c, align_bytes=64) for c in range(NCH)]
+        msg = {t: sb.tile([P, V], F32, name="msg%d" % t) for t in (1, 3, 0)}
+        msg.setdefault(2, stage.tile([P, V], F32, name="msg2", align_bytes=64, offset=LAST + 2 * V))
+        z2 = [sb.tile([P, CH, PACK], BF16, name="z2_%d" % c, align_bytes=64) for c in range(2)]
+        for c in range(2, NCH):
+            z2.append(stage.tile([P, CH, PACK], BF16, name="z2_%d" % c, align_bytes=64, offset=LAST + 4 * V * (c - 2)))
         state = {t: sb.tile([P, S], F32, name="state%d" % t) for t in (1, 3, 0)}
         low_pair = sb.tile([P, 2 * S], F32, name="low_pair")
 
@@ -175,8 +179,8 @@ def tile_picked_delivmat_none_po_kernel(
             else:
                 nc.vector.tensor_tensor(state[t][:].indirect(dst_t[:]), msg[t][:], gain_row[:], MULT)
 
-        def join(pair, t, factor):
-            nc.gpsimd.tensor_scalar(pair[:, S:], state[t][:], factor, 0.0, MULT, ADD)
+        def join(pair, t):
+            nc.gpsimd.tensor_scalar(pair[:, S:], state[t][:], gain_odd[:, t // 2 : t // 2 + 1], 0.0, MULT, ADD)
 
         def weave(copy, t, c, lo=0, hi=CH):
             copy(z2[c][:, lo:hi, t : t + 2], (state[2] if t else low_pair)[:].rearrange("p (u j) -> p j u", u=2)[:, c * CH + lo : c * CH + hi, :])
@@ -184,9 +188,14 @@ def tile_picked_delivmat_none_po_kernel(
         pieces = [slice(0, HALF), spans[2], spans[3]]
         a_first = [ps.tile([P, pieces[i].stop - pieces[i].start], F32, name="a_first%d" % i, tag="hi%d" % i) for i in range(3)]
 
+        halves = [slice(h * HALF, (h + 1) * HALF) for h in range(2)]
+        a_next = [ps.tile([P, HALF], F32, name="a_next0", tag="hi3")]
+
         def first_messages(i):
             second(a_first[i][:], 1, pieces[i])
             nc.scalar.activation(hid[1][:, pieces[i]], a_first[i][:], ACT.Tanh)
+            if i == 0:
+                second(a_next[0][:], 3, halves[0])
 
         for c in range(NCH):
             scale(c)
@@ -202,7 +211,7 @@ def tile_picked_delivmat_none_po_kernel(
         a_ps = {}
 
         def messages(t, chunks):
-            a_ps.setdefault(t, ps.tile([P, S], F32, name="a_ps%d" % t, tag="hi%d" % {3: 3, 0: 0, 2: 1}[t]))
+            a_ps.setdefault(t, ps.tile([P, S], F32, name="a_ps%d" % t, tag="hi%d" % t))
             for h in (1, 0):
                 second(a_ps[t][:, h * HALF : (h + 1) * HALF], t, slice(h * HALF, (h + 1) * HALF))
             nc.scalar.activation(hid[t][:], a_ps[t][:], ACT.Tanh)
@@ -212,25 +221,30 @@ def tile_picked_delivmat_none_po_kernel(
 
         w3 = stage.tile([P, 2 * H], U8, name="w3", align_bytes=64, offset=3072)
         deal_word_bytes(nc.vector, w3, w3_raw)
-        nc.vector.tensor_copy(msg[1][:], hid[1][:].indirect(src_t[:]))
+        nc.vector.tensor_copy(msg[1][:, : V // 2], hid[1][:].indirect(src_t[:, : V // 32]))
+        nc.scalar.activation(msg[1][:, V // 2 :], hid[1][:].indirect(src_t[:, V // 32 :]), ACT.Copy)
         deliver(1)
         s3 = stage.tile([P, H], U8, name="s3", align_bytes=64, offset=FIRST)
         deal_scales(nc.gpsimd, s3, s3_raw)
-        join(low_pair, 1, gain[:, 1:2])
+        gain_odd = stage.tile([P, 2], F32, name="gain_odd", align_bytes=64, offset=H)
+        nc.gpsimd.tensor_copy(gain_odd[:], gain[:, 1:PACK:2])
+        join(low_pair, 1)
         state.setdefault(2, stage.tile([P, 2 * S], F32, name="state2", align_bytes=64, offset=FIRST + H))
-        messages(3, [])
+        a_next.append(ps.tile([P, HALF], F32, name="a_next1", tag="hi1"))
+        second(a_next[1][:], 3, halves[1])
+        for h in range(2):
+            nc.scalar.activation(hid[3][:, halves[h]], a_next[h][:], ACT.Tanh)
+        fetch(3)
         fill(2, NCH - 1)
         fill(3, NCH - 1)
         deliver(3)
-        gain_last = stage.tile([P, 1], F32, name="gain_last", align_bytes=64, offset=H)
-        nc.gpsimd.tensor_copy(gain_last[:], gain[:, 3:4])
-        join(state[2], 3, gain_last[:])
+        join(state[2], 3)
         messages(0, [NCH - 1])
         deliver(0)
         messages(2, range(NCH - 1))
         deliver(2)
         nc.scalar.activation(low_pair[:, :S], state[0][:], ACT.Copy, scale=gain[:, 0:1])
-        for c in range(NCH):
+        for c in range(2):
             weave(nc.scalar.copy, 0, c)
 
         z2c = [sb.tile([P, CH], U32, name="z2c%d" % c, align_bytes=64) for c in range(NCH)]
@@ -252,7 +266,9 @@ def tile_picked_delivmat_none_po_kernel(
             for t in range(PACK):
                 product(nc, o_ps[c][t // 2][:, t % 2, :], w3, s3, t, z2c[c][:], z2s[c][:])
 
-        weave(nc.vector.tensor_copy, last, 0)
+        weave(nc.scalar.copy, last, 0)
+        for c in range(2, NCH):
+            weave(nc.scalar.copy, 0, c)
         weave(nc.scalar.copy, last, NCH - 1)
         for c in range(NCH):
             if c + 2 < NCH:

from contextlib import ExitStack

import concourse.mybir as mybir

K, T, S, V, H, N = 512, 2048, 512, 256, 512, 512
FLOPS = 2 * S * (K * H + H * H + H * N)

F32 = mybir.dt.float32
BF16 = mybir.dt.bfloat16
I32 = mybir.dt.int32
U32 = mybir.dt.uint32
U16 = mybir.dt.uint16
U8 = mybir.dt.uint8
FP8X4 = mybir.dt.float8_e4m3fn_x4
FP4X4 = mybir.dt.float4_e2m1fn_x4
ACT = mybir.ActivationFunctionType
MULT = mybir.AluOpType.mult
ADD = mybir.AluOpType.add

P = 128
PACK = 4
CH = 128
NCH = S // CH
HALF = 256
PICKED = 8192
FIRST = 12288
LAST = 20480


def load_scale_rows(queues, plane, scales):
    for q, queue in enumerate(queues):
        queue.dma_start(out=plane[32 * q : 32 * q + 4, :].bitcast(I32), in_=scales[0, 4 * q : 4 * q + 4, :].bitcast(I32))


def deal_word_bytes(engine, dealt, raw):
    engine.tensor_copy(
        out=dealt[:].rearrange("p (t m b) -> p t m b", t=PACK, b=2),
        in_=raw[:].rearrange("p (m t b) -> p t m b", t=PACK, b=2),
    )


def deal_scales(engine, dealt, raw):
    engine.tensor_copy(
        out=dealt[:].rearrange("p (t m) -> p t m", t=PACK),
        in_=raw[:].rearrange("p (m t) -> p t m", t=PACK),
    )


def product(nc, out, w_dealt, ws_dealt, t, codes, scales, ts=None):
    ts = t if ts is None else ts
    nc.tensor.matmul_mx(
        out=out,
        lhsT=w_dealt[:, 2 * P * t : 2 * P * (t + 1)].bitcast(FP4X4),
        lhsT_scale=ws_dealt[:, P * ts : P * (ts + 1)],
        rhs=codes.bitcast(FP8X4),
        rhs_scale=scales,
        start=True,
        stop=True,
    )


def tile_picked_delivmat_none_po_kernel(
    tc, x_words, x_scales, w1_words, w1_scales, gn, w2_words, w2_scales, w3_words, w3_scales, offs, src, dst, out_0, out_1, out_2
):
    nc = tc.nc
    with ExitStack() as ctx:
        sb = ctx.enter_context(tc.tile_pool(name="sb", bufs=1))
        stage = ctx.enter_context(tc.tile_pool(name="stage", bufs=1))
        ps = ctx.enter_context(tc.psum_pool(name="ps", bufs=1))

        offs_t = sb.tile([P, S // 16], U16, name="offs_t")
        src_t = sb.tile([P, V // 16], U16, name="src_t")
        dst_t = sb.tile([P, V // 16], U16, name="dst_t")
        xw = sb.tile([P, T], U32, name="xw", align_bytes=64)
        xs = stage.tile([P, T], U8, name="xs", align_bytes=64, offset=PICKED)
        gain = sb.tile([P, PACK], F32, name="gain")
        w1_raw = stage.tile([P, 2 * H], U8, name="w1_raw", align_bytes=64, offset=448)
        w2_raw = sb.tile([P, 2 * H], U8, name="w2_raw", align_bytes=64)
        s1_raw = sb.tile([P, H], U8, name="s1_raw", tag="s1_raw", align_bytes=64)
        w1 = sb.tile([P, 2 * H], U8, name="w1", align_bytes=64)
        w2 = sb.tile([P, 2 * H], U8, name="w2", align_bytes=64)
        s1 = [sb.tile([P, H // 2], U8, name="s1_%d" % u, align_bytes=64) for u in range(2)]
        s2 = sb.tile([P, H], U8, name="s2", align_bytes=64)

        nc.vector.memset(xs[:, : T // 2].bitcast(I32), 0)
        nc.gpsimd.memset(xs[:, T // 2 :].bitcast(I32), 0)
        nc.vector.memset(s1_raw[:].bitcast(I32), 0)

        nc.sync.dma_start(out=w1_raw[:].bitcast(I32), in_=w1_words[0].bitcast(I32))
        nc.sync.dma_start(offs_t[:], offs)
        load_scale_rows([nc.sync] * 2 + [nc.scalar] * 2, xs, x_scales)
        nc.sync.dma_start(out=xw[:].bitcast(I32), in_=x_words[0].rearrange("p c r -> p (c r)").bitcast(I32))
        load_scale_rows([nc.sync] * 4, s1_raw, w1_scales)
        nc.sync.dma_start(out=w2_raw[:].bitcast(I32), in_=w2_words[0].bitcast(I32))
        nc.sync.dma_start(out=gain[:], in_=gn.rearrange("(p t) o -> p (t o)", t=PACK))
        nc.sync.dma_start(src_t[:], src)
        nc.sync.dma_start(dst_t[:], dst)

        warm = sb.tile([P, 2], F32, name="warm")
        nc.gpsimd.memset(warm[:, 0:1], 0.0)
        nc.scalar.activation(warm[:, 1:2], warm[:, 0:1], ACT.Tanh)

        deal_word_bytes(nc.vector, w1, w1_raw)
        s2_raw = stage.tile([P, H], U8, name="s2_raw", align_bytes=64, offset=0)
        s3_raw = stage.tile([P, H], U8, name="s3_raw", align_bytes=64, offset=H)
        nc.vector.memset(s2_raw[:].bitcast(I32), 0)
        nc.vector.memset(s3_raw[:].bitcast(I32), 0)
        load_scale_rows([nc.sync] * 4, s2_raw, w2_scales)
        gs = sb.tile([P, S], U8, name="gs", align_bytes=64)
        nc.vector.tensor_copy(gs[:], xs[:].indirect(offs_t[:]))
        w3_raw = stage.tile([P, 2 * H], U8, name="w3_raw", align_bytes=64, offset=1024)
        nc.sync.dma_start(out=w3_raw[:].bitcast(I32), in_=w3_words[0].bitcast(I32))
        load_scale_rows([nc.sync] * 4, s3_raw, w3_scales)
        gw = []
        for c in range(NCH):
            gw.append(stage.tile([P, CH], U32, name="gw%d" % c, align_bytes=64, offset=PICKED + 4 * CH * (2 * (c % 2) + c // 2)))
            nc.vector.tensor_copy(gw[c][:], xw[:].indirect(offs_t[:, c * CH // 16 : (c + 1) * CH // 16]))
        for u in range(2):
            nc.gpsimd.tensor_copy(
                out=s1[u][:].rearrange("p (t m) -> p t m", t=2),
                in_=s1_raw[:].rearrange("p (m t) -> p t m", t=PACK)[:, 2 * u : 2 * u + 2],
            )
        nc.scalar.copy(
            w2[:].bitcast(U16).rearrange("p (t m) -> p t m", t=PACK),
            w2_raw[:].bitcast(U16).rearrange("p (m t) -> p t m", t=PACK),
        )
        gain_row = sb.tile([P, V], F32, name="gain_row")
        nc.scalar.copy(gain_row[:], gain[:, 2:3].to_broadcast([P, V]))
        deal_scales(nc.gpsimd, s2, s2_raw)

        spans = [slice(c * CH, (c + 1) * CH) for c in range(NCH)]
        y_ps = [ps.tile([P, PACK, CH], F32, name="y_ps%d" % c, tag="lo%d" % c) for c in range(NCH)]
        for c in range(NCH):
            for t in range(PACK):
                product(nc, y_ps[c][:, t, :], w1, s1[t // 2], t, gw[c][:], gs[:, spans[c]], t % 2)

        z_low = sb.tile([P, HALF, PACK], BF16, name="z_low", align_bytes=64)
        z = [z_low[:, :CH, :], z_low[:, CH:, :], sb.tile([P, CH, PACK], BF16, name="z2", align_bytes=64)[:]]
        z.append(stage.tile([P, CH, PACK], BF16, name="z3", align_bytes=64, offset=3584)[:])
        z_codes = [stage.tile([P, HALF], U32, name="z_codes%d" % h, align_bytes=64, offset=PICKED + 4 * HALF * h) for h in range(2)]
        z_scales = sb.tile([P, S], U8, name="z_scales", tag="z_scales", align_bytes=64)
        gain_b = gain[:].unsqueeze(1).unsqueeze(3).to_broadcast([P, CH // 2, PACK, 2])
        hid = {t: sb.tile([P, S], F32, name="hid%d" % t, align_bytes=64) for t in (0, 2, 3)}
        hid.setdefault(1, stage.tile([P, S], F32, name="hid1", align_bytes=64, offset=FIRST))
        msg = {t: sb.tile([P, V], F32, name="msg%d" % t) for t in (1, 3, 0)}
        msg.setdefault(2, stage.tile([P, V], F32, name="msg2", align_bytes=64, offset=LAST + 2 * V))
        z2 = [sb.tile([P, CH, PACK], BF16, name="z2_%d" % c, align_bytes=64) for c in range(2)]
        for c in range(2, NCH):
            z2.append(stage.tile([P, CH, PACK], BF16, name="z2_%d" % c, align_bytes=64, offset=LAST + 4 * V * (c - 2)))
        state = {t: sb.tile([P, S], F32, name="state%d" % t) for t in (1, 3, 0)}
        low_pair = sb.tile([P, 2 * S], F32, name="low_pair")

        def scale(c):
            nc.vector.tensor_tensor(
                z[c].rearrange("p (j i) t -> p j t i", i=2), y_ps[c][:].rearrange("p t (j i) -> p j t i", i=2), gain_b, MULT
            )

        def codes_of(cols):
            return z_codes[cols.start // HALF][:, cols.start % HALF : cols.start % HALF + cols.stop - cols.start]

        def quantise(values, cols):
            nc.vector.quantize_mx(out=codes_of(cols).bitcast(FP8X4), scales=z_scales[:, cols], in_=values.rearrange("p j t -> p (j t)"))

        def second(out, t, cols):
            product(nc, out, w2, s2, t, codes_of(cols), z_scales[:, cols])

        def fill(t, c):
            if t != 2:
                nc.scalar.copy(state[t][:, spans[c]], y_ps[c][:, t, :])
            else:
                nc.scalar.activation(state[t][:, spans[c]], y_ps[c][:, t, :], ACT.Copy, scale=gain[:, t : t + 1])

        def fetch(t):
            nc.scalar.activation(msg[t][:], hid[t][:].indirect(src_t[:]), ACT.Copy)

        def deliver(t):
            if t != 2:
                nc.vector.tensor_copy(state[t][:].indirect(dst_t[:]), msg[t][:])
            else:
                nc.vector.tensor_tensor(state[t][:].indirect(dst_t[:]), msg[t][:], gain_row[:], MULT)

        def join(pair, t):
            nc.gpsimd.tensor_scalar(pair[:, S:], state[t][:], gain_odd[:, t // 2 : t // 2 + 1], 0.0, MULT, ADD)

        def weave(copy, t, c, lo=0, hi=CH):
            copy(z2[c][:, lo:hi, t : t + 2], (state[2] if t else low_pair)[:].rearrange("p (u j) -> p j u", u=2)[:, c * CH + lo : c * CH + hi, :])

        pieces = [slice(0, HALF), spans[2], spans[3]]
        a_first = [ps.tile([P, pieces[i].stop - pieces[i].start], F32, name="a_first%d" % i, tag="hi%d" % i) for i in range(3)]

        halves = [slice(h * HALF, (h + 1) * HALF) for h in range(2)]
        a_next = [ps.tile([P, HALF], F32, name="a_next0", tag="hi3")]

        def first_messages(i):
            second(a_first[i][:], 1, pieces[i])
            nc.scalar.activation(hid[1][:, pieces[i]], a_first[i][:], ACT.Tanh)
            if i == 0:
                second(a_next[0][:], 3, halves[0])

        for c in range(NCH):
            scale(c)
            if c >= 2:
                quantise((z_low[:], z[2])[c - 2], pieces[c - 2])
                first_messages(c - 2)
            fill(1, c)
            if c < NCH - 1:
                fill(3, c)
                fill(0, c)
        quantise(z[3], pieces[2])
        first_messages(2)
        a_ps = {}

        def messages(t, chunks):
            a_ps.setdefault(t, ps.tile([P, S], F32, name="a_ps%d" % t, tag="hi%d" % t))
            for h in (1, 0):
                second(a_ps[t][:, h * HALF : (h + 1) * HALF], t, slice(h * HALF, (h + 1) * HALF))
            nc.scalar.activation(hid[t][:], a_ps[t][:], ACT.Tanh)
            fetch(t)
            for c in chunks:
                fill(t, c)

        w3 = stage.tile([P, 2 * H], U8, name="w3", align_bytes=64, offset=3072)
        deal_word_bytes(nc.vector, w3, w3_raw)
        nc.vector.tensor_copy(msg[1][:, : V // 2], hid[1][:].indirect(src_t[:, : V // 32]))
        nc.scalar.activation(msg[1][:, V // 2 :], hid[1][:].indirect(src_t[:, V // 32 :]), ACT.Copy)
        deliver(1)
        s3 = stage.tile([P, H], U8, name="s3", align_bytes=64, offset=FIRST)
        deal_scales(nc.gpsimd, s3, s3_raw)
        gain_odd = stage.tile([P, 2], F32, name="gain_odd", align_bytes=64, offset=H)
        nc.gpsimd.tensor_copy(gain_odd[:], gain[:, 1:PACK:2])
        join(low_pair, 1)
        state.setdefault(2, stage.tile([P, 2 * S], F32, name="state2", align_bytes=64, offset=FIRST + H))
        a_next.append(ps.tile([P, HALF], F32, name="a_next1", tag="hi1"))
        second(a_next[1][:], 3, halves[1])
        for h in range(2):
            nc.scalar.activation(hid[3][:, halves[h]], a_next[h][:], ACT.Tanh)
        fetch(3)
        fill(2, NCH - 1)
        fill(3, NCH - 1)
        deliver(3)
        join(state[2], 3)
        messages(0, [NCH - 1])
        deliver(0)
        messages(2, range(NCH - 1))
        deliver(2)
        nc.scalar.activation(low_pair[:, :S], state[0][:], ACT.Copy, scale=gain[:, 0:1])
        for c in range(2):
            weave(nc.scalar.copy, 0, c)

        z2c = [sb.tile([P, CH], U32, name="z2c%d" % c, align_bytes=64) for c in range(NCH)]
        z2s = [sb.tile([P, CH], U8, name="z2s%d" % c, align_bytes=64) for c in range(NCH)]
        o_ps = [
            [ps.tile([P, 2, CH], F32, name="o_ps%d_%d" % (c, u), tag=("lo%d", "hi%d")[u] % c) for u in range(2)] for c in range(NCH)
        ]
        o_late = sb.tile([P, PACK, HALF], F32, name="o_late")
        o32 = [sb.tile([P, PACK, CH], F32, name="o32_%d" % c)[:] for c in range(2)] + [o_late[:, :, :CH], o_late[:, :, CH:]]
        o16 = [sb.tile([P, CH, PACK], BF16, name="o16_%d" % c, align_bytes=64) for c in range(NCH)]
        oc = sb.tile([P, S], U32, name="oc", align_bytes=64)
        osc = sb.tile([P, S], U8, name="osc", align_bytes=64)
        out_rows = out_0.rearrange("(p t) j -> p t j", t=PACK)
        out_words = out_1[0].rearrange("p c r -> p (c r)").bitcast(I32)
        last = 2

        def third(c):
            nc.vector.quantize_mx(out=z2c[c][:].bitcast(FP8X4), scales=z2s[c][:], in_=z2[c][:].rearrange("p j t -> p (j t)"))
            for t in range(PACK):
                product(nc, o_ps[c][t // 2][:, t % 2, :], w3, s3, t, z2c[c][:], z2s[c][:])

        weave(nc.scalar.copy, last, 0)
        for c in range(2, NCH):
            weave(nc.scalar.copy, 0, c)
        weave(nc.scalar.copy, last, NCH - 1)
        for c in range(NCH):
            if c + 2 < NCH:
                weave(nc.vector.tensor_copy, last, c + 1)
            third(c)
        for c in range(NCH):
            cols = spans[c]
            for u in range(2):
                copy = nc.vector.tensor_copy if (c, u) == (1, 0) else nc.scalar.copy
                copy(o32[c][:, 2 * u : 2 * u + 2, :], o_ps[c][u][:])
                if c == 0:
                    nc.sync.dma_start(out=out_rows[:, 2 * u : 2 * u + 2, cols], in_=o32[c][:, 2 * u : 2 * u + 2, :])
                if c == NCH - 1:
                    nc.sync.dma_start(out=out_rows[:, 2 * u : 2 * u + 2, HALF:], in_=o_late[:, 2 * u : 2 * u + 2, :])
            if c == 1:
                nc.sync.dma_start(out=out_rows[:, :, cols], in_=o32[c])
            nc.vector.tensor_copy(
                out=o16[c][:].rearrange("p (j i) t -> p j t i", i=4),
                in_=o32[c].rearrange("p t (j i) -> p j t i", i=4),
            )
            nc.vector.quantize_mx(out=oc[:, cols].bitcast(FP8X4), scales=osc[:, cols], in_=o16[c][:].rearrange("p j t -> p (j t)"))
        nc.sync.dma_start(out=out_words, in_=oc[:].bitcast(I32))
        for q in range(4):
            queue = nc.sync if q == 0 else nc.scalar
            queue.dma_start(out=out_2[0, 4 * q : 4 * q + 4, :].bitcast(I32), in_=osc[32 * q : 32 * q + 4, :].bitcast(I32))
